import numpy as np
import ml_dtypes


def mxq(x, axis, fmt="e4m3"):
    dtype, down = {"e4m3": (ml_dtypes.float8_e4m3fn, 7), "e5m2": (ml_dtypes.float8_e5m2, 14)}[fmt]
    v = np.moveaxis(np.asarray(x, np.float32).astype(ml_dtypes.bfloat16).astype(np.float64), axis, -1)
    blocks = v.reshape(v.shape[:-1] + (-1, 32))
    amax = np.abs(blocks).max(-1, keepdims=True)
    byte = np.maximum(np.where(amax > 0, np.frexp(amax)[1] - 1 + 127, 0) - down, 1)
    scale = np.exp2(byte - 127.0)
    codes = (blocks / scale).astype(np.float32).astype(dtype).astype(np.float64)
    return np.moveaxis((codes * scale).reshape(v.shape), -1, axis)


WIDE = False


def mx_kscale(k):
    if not WIDE:
        return np.ones(k)
    levels = np.array([10, -10, 5, -5, 0])
    if k % 512:
        return np.exp2(np.random.permutation(np.resize(levels, k // 32))).repeat(32)
    a = np.empty((k // 512, 16))
    for p in range(k // 512):
        a[p, :8] = np.random.permutation(np.resize(levels, 8))
        for g in range(8):
            far = levels[np.abs(levels - a[p, g]) >= 10]
            a[p, g + 8] = far[np.random.randint(len(far))]
    return np.exp2(a.ravel()).repeat(32)


def f64(x):
    return np.asarray(x).astype(np.float64)


def striped(idx):
    return np.tile(idx.reshape(-1, 16).T, (8, 1)).astype(np.uint16)


def unstriped(offs):
    return offs[:16].T.reshape(-1).astype(np.int64)


def pack_weight(w):
    k, n = w.shape
    w = f64(np.asarray(w, np.float32).astype(ml_dtypes.bfloat16)).reshape(k // 32, 32, n)
    amax = np.abs(w).max(1)
    byte = np.clip(np.where(amax > 0, np.frexp(amax)[1] - 1 + 127 - 7, 1), 1, 254)
    scaled = (w * np.exp2(127.0 - byte)[:, None, :]).reshape(k, n).astype(np.float32)
    words = np.ascontiguousarray(scaled.reshape(k // 512, 128, 4, n).transpose(0, 1, 3, 2)).astype(ml_dtypes.float8_e4m3fn).view(np.uint8)
    return words, np.ascontiguousarray(byte.astype(np.uint8).reshape(k // 512, 16, n))


def unpack_weight(words, scales):
    g, p, n, _ = words.shape
    vals = np.ascontiguousarray(words).view(ml_dtypes.float8_e4m3fn).astype(np.float64) * np.repeat(np.exp2(scales.astype(np.float64) - 127.0), 8, axis=1)[..., None]
    return vals.transpose(0, 1, 3, 2).reshape(g * 512, n)


K, T, S, N, U = 512, 2048, 1024, 128, 1024


def setup_inputs():
    n = np.random.standard_normal
    s = mx_kscale(K)[:, None]
    packed_xT = pack_weight(n((K, T)) * s)
    return {
        "x_words": packed_xT[0],
        "x_scales": packed_xT[1],
        "w1": (n((K, N)) / np.sqrt(K) / s).astype(np.float32),
        "gamma": np.random.uniform(0.5, 1.5, (N, U)).astype(np.float32),
        "beta": (0.5 * n((N, U))).astype(np.float32),
        "offs": striped(np.random.permutation(T)[:S]),
        "cls": striped(np.random.randint(0, U, S)),
    }


def reference(x_words, x_scales, w1, gamma, beta, offs, cls):
    xq = unpack_weight(x_words, x_scales)[:, unstriped(offs)]
    y = mxq(f64(w1), 0, "e4m3").T @ xq
    g = f64(gamma)[:, unstriped(cls)]
    s = f64(beta)[:, unstriped(cls)]
    return y * g + s

@@ -1,0 +1,94 @@
+from contextlib import ExitStack
+
+import concourse.mybir as mybir
+
+K, T, S, N, U = 512, 2048, 1024, 128, 1024
+FLOPS = 2 * K * N * S
+
+F32 = mybir.dt.float32
+BF16 = mybir.dt.bfloat16
+I32 = mybir.dt.int32
+U32 = mybir.dt.uint32
+U16 = mybir.dt.uint16
+U8 = mybir.dt.uint8
+FP8X4 = mybir.dt.float8_e4m3fn_x4
+MULT = mybir.AluOpType.mult
+ADD = mybir.AluOpType.add
+
+P = 128
+PACK = 4
+STRIPE = 16
+PIECES = ((0, 256), (256, 768), (768, 1024))
+
+
+def tile_picked_cbn_none_p_kernel(tc, x_words, x_scales, w1, gamma, beta, offs, cls, out):
+    nc = tc.nc
+    with ExitStack() as ctx:
+        keep = ctx.enter_context(tc.tile_pool(name="keep", bufs=1))
+        psum = ctx.enter_context(tc.psum_pool(name="psum", bufs=1))
+
+        offs_sb = keep.tile([P, S // STRIPE], U16)
+        cls_sb = keep.tile([P, S // STRIPE], U16)
+        w_raw = keep.tile([P, PACK, N], F32)
+        scale_table = keep.tile([P, T], U8)
+        word_table = keep.tile([P, T], I32)
+        gamma_sb = keep.tile([P, U], F32)
+        beta_sb = keep.tile([P, U], F32)
+
+        nc.vector.memset(scale_table[:].bitcast(I32), 0)
+        nc.sync.dma_start(offs_sb[:], offs)
+        nc.sync.dma_start(w_raw[:], w1.rearrange("(p j) m -> p j m", j=PACK))
+        for q in range(4):
+            nc.sync.dma_start(scale_table[32 * q : 32 * q + 4, :].bitcast(I32), x_scales[0, 4 * q : 4 * q + 4, :].bitcast(I32))
+        nc.sync.dma_start(word_table[:], x_words[0].rearrange("p n t -> p (n t)").bitcast(I32))
+        nc.sync.dma_start(cls_sb[:], cls)
+        nc.sync.dma_start(gamma_sb[:], gamma)
+        nc.sync.dma_start(beta_sb[:], beta)
+
+        w_grouped = keep.tile([P, N, PACK], BF16, align_bytes=64)
+        nc.scalar.copy(w_grouped[:], w_raw[:].rearrange("p j m -> p m j"))
+
+        x_bytes = keep.tile([P, S], U8, align_bytes=64)
+        nc.vector.tensor_copy(x_bytes[:], scale_table[:].indirect(offs_sb[:]))
+
+        w_codes = keep.tile([P, N], U32, align_bytes=64)
+        w_bytes = keep.tile([P, N], U8, align_bytes=64)
+        nc.vector.quantize_mx(w_codes[:].bitcast(FP8X4), w_bytes[:], w_grouped[:].rearrange("p m j -> p (m j)"))
+
+        ys = []
+        for i, (a, b) in enumerate(PIECES):
+            codes = keep.tile([P, b - a], U32, align_bytes=64, name=f"codes{i}")
+            nc.vector.tensor_copy(codes[:], word_table[:].bitcast(U32).indirect(offs_sb[:, a // STRIPE : b // STRIPE]))
+            acc = psum.tile([N, b - a], F32, name=f"acc{i}")
+            nc.tensor.matmul_mx(
+                out=acc[:],
+                lhsT=w_codes[:].bitcast(FP8X4),
+                lhsT_scale=w_bytes[:],
+                rhs=codes[:].bitcast(FP8X4),
+                rhs_scale=x_bytes[:, a:b],
+                start=True,
+                stop=True,
+            )
+            y = keep.tile([N, b - a], F32, name=f"y{i}")
+            nc.scalar.copy(y[:], acc[:])
+            ys.append(y)
+
+        scaled = []
+
+        def scale(i):
+            a, b = PIECES[i]
+            z = keep.tile([N, b - a], F32, name=f"z{i}")
+            nc.vector.tensor_tensor(z[:], gamma_sb[:].indirect(cls_sb[:, a // STRIPE : b // STRIPE]), ys[i][:], MULT)
+            scaled.append(z)
+
+        def shift(i):
+            a, b = PIECES[i]
+            r = keep.tile([N, b - a], F32, name=f"r{i}")
+            nc.vector.tensor_tensor(r[:], beta_sb[:].indirect(cls_sb[:, a // STRIPE : b // STRIPE]), scaled[i][:], ADD)
+            nc.sync.dma_start(out[:, a:b], r[:])
+
+        scale(0)
+        for i in range(1, len(PIECES)):
+            scale(i)
+            shift(i - 1)
+        shift(len(PIECES) - 1)

@@ -18,7 +18,9 @@ ADD = mybir.AluOpType.add
 P = 128
 PACK = 4
 STRIPE = 16
-PIECES = ((0, 256), (256, 768), (768, 1024))
+PRODUCTS = ((0, 256), (256, 512), (512, 768), (768, 1024))
+SCALINGS = ((0, 512), (512, 768), (768, 1024))
+SHIFTS = ((0, 512), (512, 768), (768, 1024))
 
 
 def tile_picked_cbn_none_p_kernel(tc, x_words, x_scales, w1, gamma, beta, offs, cls, out):
@@ -35,28 +37,32 @@ def tile_picked_cbn_none_p_kernel(tc, x_words, x_scales, w1, gamma, beta, offs, 
         gamma_sb = keep.tile([P, U], F32)
         beta_sb = keep.tile([P, U], F32)
 
+        def load_scales(queue, q):
+            queue.dma_start(scale_table[q:P:32, :].bitcast(I32), x_scales[0, q:16:4, :].bitcast(I32))
+
         nc.vector.memset(scale_table[:].bitcast(I32), 0)
-        nc.sync.dma_start(offs_sb[:], offs)
         nc.sync.dma_start(w_raw[:], w1.rearrange("(p j) m -> p j m", j=PACK))
-        for q in range(4):
-            nc.sync.dma_start(scale_table[32 * q : 32 * q + 4, :].bitcast(I32), x_scales[0, 4 * q : 4 * q + 4, :].bitcast(I32))
+        nc.sync.dma_start(offs_sb[:], offs)
+        load_scales(nc.sync, 0)
+        load_scales(nc.sync, 1)
+        load_scales(nc.sync, 2)
+        load_scales(nc.sync, 3)
         nc.sync.dma_start(word_table[:], x_words[0].rearrange("p n t -> p (n t)").bitcast(I32))
         nc.sync.dma_start(cls_sb[:], cls)
         nc.sync.dma_start(gamma_sb[:], gamma)
         nc.sync.dma_start(beta_sb[:], beta)
 
         w_grouped = keep.tile([P, N, PACK], BF16, align_bytes=64)
-        nc.scalar.copy(w_grouped[:], w_raw[:].rearrange("p j m -> p m j"))
-
-        x_bytes = keep.tile([P, S], U8, align_bytes=64)
-        nc.vector.tensor_copy(x_bytes[:], scale_table[:].indirect(offs_sb[:]))
-
+        nc.vector.tensor_copy(w_grouped[:], w_raw[:].rearrange("p j m -> p m j"))
         w_codes = keep.tile([P, N], U32, align_bytes=64)
         w_bytes = keep.tile([P, N], U8, align_bytes=64)
         nc.vector.quantize_mx(w_codes[:].bitcast(FP8X4), w_bytes[:], w_grouped[:].rearrange("p m j -> p (m j)"))
 
-        ys = []
-        for i, (a, b) in enumerate(PIECES):
+        x_bytes = keep.tile([P, S], U8, align_bytes=64)
+        nc.vector.tensor_copy(x_bytes[:], scale_table[:].indirect(offs_sb[:]))
+
+        y = keep.tile([N, S], F32)
+        for i, (a, b) in enumerate(PRODUCTS):
             codes = keep.tile([P, b - a], U32, align_bytes=64, name=f"codes{i}")
             nc.vector.tensor_copy(codes[:], word_table[:].bitcast(U32).indirect(offs_sb[:, a // STRIPE : b // STRIPE]))
             acc = psum.tile([N, b - a], F32, name=f"acc{i}")
@@ -69,26 +75,12 @@ def tile_picked_cbn_none_p_kernel(tc, x_words, x_scales, w1, gamma, beta, offs, 
                 start=True,
                 stop=True,
             )
-            y = keep.tile([N, b - a], F32, name=f"y{i}")
-            nc.scalar.copy(y[:], acc[:])
-            ys.append(y)
+            nc.scalar.copy(y[:, a:b], acc[:])
 
-        scaled = []
-
-        def scale(i):
-            a, b = PIECES[i]
-            z = keep.tile([N, b - a], F32, name=f"z{i}")
-            nc.vector.tensor_tensor(z[:], gamma_sb[:].indirect(cls_sb[:, a // STRIPE : b // STRIPE]), ys[i][:], MULT)
-            scaled.append(z)
-
-        def shift(i):
-            a, b = PIECES[i]
-            r = keep.tile([N, b - a], F32, name=f"r{i}")
-            nc.vector.tensor_tensor(r[:], beta_sb[:].indirect(cls_sb[:, a // STRIPE : b // STRIPE]), scaled[i][:], ADD)
-            nc.sync.dma_start(out[:, a:b], r[:])
-
-        scale(0)
-        for i in range(1, len(PIECES)):
-            scale(i)
-            shift(i - 1)
-        shift(len(PIECES) - 1)
+        z = keep.tile([N, S], F32)
+        for a, b in SCALINGS:
+            nc.vector.tensor_tensor(z[:, a:b], gamma_sb[:].indirect(cls_sb[:, a // STRIPE : b // STRIPE]), y[:, a:b], MULT)
+        result = keep.tile([N, S], F32)
+        for a, b in SHIFTS:
+            nc.vector.tensor_tensor(result[:, a:b], beta_sb[:].indirect(cls_sb[:, a // STRIPE : b // STRIPE]), z[:, a:b], ADD)
+            nc.sync.dma_start(out[:, a:b], result[:, a:b])

@@ -19,8 +19,8 @@ P = 128
 PACK = 4
 STRIPE = 16
 PRODUCTS = ((0, 256), (256, 512), (512, 768), (768, 1024))
-SCALINGS = ((0, 512), (512, 768), (768, 1024))
-SHIFTS = ((0, 512), (512, 768), (768, 1024))
+SCALINGS = ((0, 256), (256, 512), (512, 768), (768, 1024))
+SHIFTS = ((0, 512), (512, 768), (768, 896), (896, 1024))
 
 
 def tile_picked_cbn_none_p_kernel(tc, x_words, x_scales, w1, gamma, beta, offs, cls, out):
@@ -43,9 +43,9 @@ def tile_picked_cbn_none_p_kernel(tc, x_words, x_scales, w1, gamma, beta, offs, 
         nc.vector.memset(scale_table[:].bitcast(I32), 0)
         nc.sync.dma_start(w_raw[:], w1.rearrange("(p j) m -> p j m", j=PACK))
         nc.sync.dma_start(offs_sb[:], offs)
-        load_scales(nc.sync, 0)
+        load_scales(nc.scalar, 0)
         load_scales(nc.sync, 1)
-        load_scales(nc.sync, 2)
+        load_scales(nc.scalar, 2)
         load_scales(nc.sync, 3)
         nc.sync.dma_start(word_table[:], x_words[0].rearrange("p n t -> p (n t)").bitcast(I32))
         nc.sync.dma_start(cls_sb[:], cls)

@@ -17,14 +17,18 @@ ADD = mybir.AluOpType.add
 
 P = 128
 PACK = 4
+QUADRANT = 32
+SCALE_ROWS = 4
 STRIPE = 16
-PRODUCTS = ((0, 256), (256, 512), (512, 768), (768, 1024))
-SCALINGS = ((0, 256), (256, 512), (512, 768), (768, 1024))
+
+PIECE = 256
 SHIFTS = ((0, 512), (512, 768), (768, 896), (896, 1024))
 
 
 def tile_picked_cbn_none_p_kernel(tc, x_words, x_scales, w1, gamma, beta, offs, cls, out):
     nc = tc.nc
+    pieces = [(a, a + PIECE) for a in range(0, S, PIECE)]
+
     with ExitStack() as ctx:
         keep = ctx.enter_context(tc.tile_pool(name="keep", bufs=1))
         psum = ctx.enter_context(tc.psum_pool(name="psum", bufs=1))
@@ -37,16 +41,15 @@ def tile_picked_cbn_none_p_kernel(tc, x_words, x_scales, w1, gamma, beta, offs, 
         gamma_sb = keep.tile([P, U], F32)
         beta_sb = keep.tile([P, U], F32)
 
-        def load_scales(queue, q):
-            queue.dma_start(scale_table[q:P:32, :].bitcast(I32), x_scales[0, q:16:4, :].bitcast(I32))
-
         nc.vector.memset(scale_table[:].bitcast(I32), 0)
+
         nc.sync.dma_start(w_raw[:], w1.rearrange("(p j) m -> p j m", j=PACK))
         nc.sync.dma_start(offs_sb[:], offs)
-        load_scales(nc.scalar, 0)
-        load_scales(nc.sync, 1)
-        load_scales(nc.scalar, 2)
-        load_scales(nc.sync, 3)
+        for r in range(SCALE_ROWS):
+            nc.sync.dma_start(
+                scale_table[r:P:QUADRANT, :].bitcast(I32),
+                x_scales[0, r : K // 32 : SCALE_ROWS, :].bitcast(I32),
+            )
         nc.sync.dma_start(word_table[:], x_words[0].rearrange("p n t -> p (n t)").bitcast(I32))
         nc.sync.dma_start(cls_sb[:], cls)
         nc.sync.dma_start(gamma_sb[:], gamma)
@@ -62,25 +65,26 @@ def tile_picked_cbn_none_p_kernel(tc, x_words, x_scales, w1, gamma, beta, offs, 
         nc.vector.tensor_copy(x_bytes[:], scale_table[:].indirect(offs_sb[:]))
 
         y = keep.tile([N, S], F32)
-        for i, (a, b) in enumerate(PRODUCTS):
-            codes = keep.tile([P, b - a], U32, align_bytes=64, name=f"codes{i}")
-            nc.vector.tensor_copy(codes[:], word_table[:].bitcast(U32).indirect(offs_sb[:, a // STRIPE : b // STRIPE]))
-            acc = psum.tile([N, b - a], F32, name=f"acc{i}")
+        for i, (a, b) in enumerate(pieces):
+            x_codes = keep.tile([P, PIECE], U32, align_bytes=64, name=f"x_codes{i}")
+            nc.vector.tensor_copy(x_codes[:], word_table[:].bitcast(U32).indirect(offs_sb[:, a // STRIPE : b // STRIPE]))
+            acc = psum.tile([N, PIECE], F32, name=f"acc{i}")
             nc.tensor.matmul_mx(
                 out=acc[:],
                 lhsT=w_codes[:].bitcast(FP8X4),
                 lhsT_scale=w_bytes[:],
-                rhs=codes[:].bitcast(FP8X4),
+                rhs=x_codes[:].bitcast(FP8X4),
                 rhs_scale=x_bytes[:, a:b],
                 start=True,
                 stop=True,
             )
             nc.scalar.copy(y[:, a:b], acc[:])
 
-        z = keep.tile([N, S], F32)
-        for a, b in SCALINGS:
-            nc.vector.tensor_tensor(z[:, a:b], gamma_sb[:].indirect(cls_sb[:, a // STRIPE : b // STRIPE]), y[:, a:b], MULT)
+        scaled = keep.tile([N, S], F32)
+        for a, b in pieces:
+            nc.vector.tensor_tensor(scaled[:, a:b], gamma_sb[:].indirect(cls_sb[:, a // STRIPE : b // STRIPE]), y[:, a:b], MULT)
+
         result = keep.tile([N, S], F32)
         for a, b in SHIFTS:
-            nc.vector.tensor_tensor(result[:, a:b], beta_sb[:].indirect(cls_sb[:, a // STRIPE : b // STRIPE]), z[:, a:b], ADD)
+            nc.vector.tensor_tensor(result[:, a:b], beta_sb[:].indirect(cls_sb[:, a // STRIPE : b // STRIPE]), scaled[:, a:b], ADD)
             nc.sync.dma_start(out[:, a:b], result[:, a:b])

@@ -36,33 +36,39 @@ def tile_picked_cbn_none_p_kernel(tc, x_words, x_scales, w1, gamma, beta, offs, 
         offs_sb = keep.tile([P, S // STRIPE], U16)
         cls_sb = keep.tile([P, S // STRIPE], U16)
         w_raw = keep.tile([P, PACK, N], F32)
-        scale_table = keep.tile([P, T], U8)
+        scale_table = keep.tile([P, T], U8, tag="early_then_beta")
         word_table = keep.tile([P, T], I32)
         gamma_sb = keep.tile([P, U], F32)
-        beta_sb = keep.tile([P, U], F32)
+        x_bytes = keep.tile([P, S], U8, align_bytes=64)
 
         nc.vector.memset(scale_table[:].bitcast(I32), 0)
+        nc.vector.memset(x_bytes[:].bitcast(I32), 0)
 
-        nc.sync.dma_start(w_raw[:], w1.rearrange("(p j) m -> p j m", j=PACK))
         nc.sync.dma_start(offs_sb[:], offs)
-        for r in range(SCALE_ROWS):
-            nc.sync.dma_start(
-                scale_table[r:P:QUADRANT, :].bitcast(I32),
-                x_scales[0, r : K // 32 : SCALE_ROWS, :].bitcast(I32),
-            )
+        nc.sync.dma_start(w_raw[:], w1.rearrange("(p j) m -> p j m", j=PACK))
+        nc.sync.dma_start(scale_table[0:P:8, :].bitcast(I32), x_scales[0].bitcast(I32))
         nc.sync.dma_start(word_table[:], x_words[0].rearrange("p n t -> p (n t)").bitcast(I32))
         nc.sync.dma_start(cls_sb[:], cls)
         nc.sync.dma_start(gamma_sb[:], gamma)
-        nc.sync.dma_start(beta_sb[:], beta)
 
         w_grouped = keep.tile([P, N, PACK], BF16, align_bytes=64)
-        nc.vector.tensor_copy(w_grouped[:], w_raw[:].rearrange("p j m -> p m j"))
+        nc.scalar.copy(w_grouped[:], w_raw[:].rearrange("p j m -> p m j"))
+
+        for i, (a, b) in enumerate(((0, S // 2), (S // 2, S))):
+            picked = keep.tile([P, S // 2], U8, align_bytes=64, name=f"picked{i}")
+            nc.vector.tensor_copy(picked[:], scale_table[:].indirect(offs_sb[:, a // STRIPE : b // STRIPE]))
+            for r in range(SCALE_ROWS):
+                nc.sync.dma_start(
+                    x_bytes[r:P:QUADRANT, a:b].bitcast(I32),
+                    picked[8 * r : P : QUADRANT, :].bitcast(I32),
+                )
+
+        beta_sb = keep.tile([P, U], F32, tag="early_then_beta")
+        nc.sync.dma_start(beta_sb[:], beta)
+
         w_codes = keep.tile([P, N], U32, align_bytes=64)
         w_bytes = keep.tile([P, N], U8, align_bytes=64)
         nc.vector.quantize_mx(w_codes[:].bitcast(FP8X4), w_bytes[:], w_grouped[:].rearrange("p m j -> p (m j)"))
-
-        x_bytes = keep.tile([P, S], U8, align_bytes=64)
-        nc.vector.tensor_copy(x_bytes[:], scale_table[:].indirect(offs_sb[:]))
 
         y = keep.tile([N, S], F32)
         for i, (a, b) in enumerate(pieces):

@@ -41,12 +41,16 @@ def tile_picked_cbn_none_p_kernel(tc, x_words, x_scales, w1, gamma, beta, offs, 
         gamma_sb = keep.tile([P, U], F32)
         x_bytes = keep.tile([P, S], U8, align_bytes=64)
 
-        nc.vector.memset(scale_table[:].bitcast(I32), 0)
+        nc.vector.memset(scale_table[32:64, :].bitcast(I32), 0)
+        nc.vector.memset(scale_table[64:P, :].bitcast(I32), 0)
         nc.vector.memset(x_bytes[:].bitcast(I32), 0)
 
         nc.sync.dma_start(offs_sb[:], offs)
+        nc.sync.dma_start(
+            scale_table[0:QUADRANT, :].bitcast(I32),
+            x_scales.rearrange("z q c -> q z c").bitcast(I32).to_broadcast([K // 32, 2, T // 4]),
+        )
         nc.sync.dma_start(w_raw[:], w1.rearrange("(p j) m -> p j m", j=PACK))
-        nc.sync.dma_start(scale_table[0:P:8, :].bitcast(I32), x_scales[0].bitcast(I32))
         nc.sync.dma_start(word_table[:], x_words[0].rearrange("p n t -> p (n t)").bitcast(I32))
         nc.sync.dma_start(cls_sb[:], cls)
         nc.sync.dma_start(gamma_sb[:], gamma)
@@ -54,13 +58,13 @@ def tile_picked_cbn_none_p_kernel(tc, x_words, x_scales, w1, gamma, beta, offs, 
         w_grouped = keep.tile([P, N, PACK], BF16, align_bytes=64)
         nc.scalar.copy(w_grouped[:], w_raw[:].rearrange("p j m -> p m j"))
 
-        for i, (a, b) in enumerate(((0, S // 2), (S // 2, S))):
-            picked = keep.tile([P, S // 2], U8, align_bytes=64, name=f"picked{i}")
+        for i, (a, b) in enumerate(((0, S - PIECE), (S - PIECE, S))):
+            picked = keep.tile([P, b - a], U8, align_bytes=64, name=f"picked{i}")
             nc.vector.tensor_copy(picked[:], scale_table[:].indirect(offs_sb[:, a // STRIPE : b // STRIPE]))
             for r in range(SCALE_ROWS):
-                nc.sync.dma_start(
+                (nc.scalar if i == 0 and r % 2 else nc.sync).dma_start(
                     x_bytes[r:P:QUADRANT, a:b].bitcast(I32),
-                    picked[8 * r : P : QUADRANT, :].bitcast(I32),
+                    picked[2 * r + i : QUADRANT : 8, :].bitcast(I32),
                 )
 
         beta_sb = keep.tile([P, U], F32, tag="early_then_beta")

@@ -35,10 +35,9 @@ def tile_picked_cbn_none_p_kernel(tc, x_words, x_scales, w1, gamma, beta, offs, 
 
         offs_sb = keep.tile([P, S // STRIPE], U16)
         cls_sb = keep.tile([P, S // STRIPE], U16)
-        w_raw = keep.tile([P, PACK, N], F32)
+        w_raw = keep.tile([P, PACK, N], F32, tag="w_then_gamma")
         scale_table = keep.tile([P, T], U8, tag="early_then_beta")
         word_table = keep.tile([P, T], I32)
-        gamma_sb = keep.tile([P, U], F32)
         x_bytes = keep.tile([P, S], U8, align_bytes=64)
 
         nc.vector.memset(scale_table[32:64, :].bitcast(I32), 0)
@@ -53,19 +52,21 @@ def tile_picked_cbn_none_p_kernel(tc, x_words, x_scales, w1, gamma, beta, offs, 
         nc.sync.dma_start(w_raw[:], w1.rearrange("(p j) m -> p j m", j=PACK))
         nc.sync.dma_start(word_table[:], x_words[0].rearrange("p n t -> p (n t)").bitcast(I32))
         nc.sync.dma_start(cls_sb[:], cls)
-        nc.sync.dma_start(gamma_sb[:], gamma)
 
         w_grouped = keep.tile([P, N, PACK], BF16, align_bytes=64)
         nc.scalar.copy(w_grouped[:], w_raw[:].rearrange("p j m -> p m j"))
 
-        for i, (a, b) in enumerate(((0, S - PIECE), (S - PIECE, S))):
+        for i, (a, b) in enumerate(((0, S // 2), (S // 2, S))):
             picked = keep.tile([P, b - a], U8, align_bytes=64, name=f"picked{i}")
             nc.vector.tensor_copy(picked[:], scale_table[:].indirect(offs_sb[:, a // STRIPE : b // STRIPE]))
             for r in range(SCALE_ROWS):
-                (nc.scalar if i == 0 and r % 2 else nc.sync).dma_start(
+                nc.sync.dma_start(
                     x_bytes[r:P:QUADRANT, a:b].bitcast(I32),
                     picked[2 * r + i : QUADRANT : 8, :].bitcast(I32),
                 )
+            if i == 0:
+                gamma_sb = keep.tile([P, U], F32, tag="w_then_gamma")
+                nc.sync.dma_start(gamma_sb[:], gamma)
 
         beta_sb = keep.tile([P, U], F32, tag="early_then_beta")
         nc.sync.dma_start(beta_sb[:], beta)

@@ -17,8 +17,10 @@ ADD = mybir.AluOpType.add
 
 P = 128
 PACK = 4
+BLOCKS = K // 32
 QUADRANT = 32
 SCALE_ROWS = 4
+COPIES = QUADRANT // BLOCKS
 STRIPE = 16
 
 PIECE = 256
@@ -27,7 +29,7 @@ SHIFTS = ((0, 512), (512, 768), (768, 896), (896, 1024))
 
 def tile_picked_cbn_none_p_kernel(tc, x_words, x_scales, w1, gamma, beta, offs, cls, out):
     nc = tc.nc
-    pieces = [(a, a + PIECE) for a in range(0, S, PIECE)]
+    pieces = [(start, start + PIECE) for start in range(0, S, PIECE)]
 
     with ExitStack() as ctx:
         keep = ctx.enter_context(tc.tile_pool(name="keep", bufs=1))
@@ -36,19 +38,19 @@ def tile_picked_cbn_none_p_kernel(tc, x_words, x_scales, w1, gamma, beta, offs, 
         offs_sb = keep.tile([P, S // STRIPE], U16)
         cls_sb = keep.tile([P, S // STRIPE], U16)
         w_raw = keep.tile([P, PACK, N], F32, tag="w_then_gamma")
-        scale_table = keep.tile([P, T], U8, tag="early_then_beta")
+        scale_table = keep.tile([P, T], U8, tag="scales_then_beta")
         word_table = keep.tile([P, T], I32)
         x_bytes = keep.tile([P, S], U8, align_bytes=64)
 
-        nc.vector.memset(scale_table[32:64, :].bitcast(I32), 0)
-        nc.vector.memset(scale_table[64:P, :].bitcast(I32), 0)
+        nc.vector.memset(scale_table[QUADRANT : 2 * QUADRANT, :].bitcast(I32), 0)
+        nc.vector.memset(scale_table[2 * QUADRANT : P, :].bitcast(I32), 0)
         nc.vector.memset(x_bytes[:].bitcast(I32), 0)
 
-        nc.sync.dma_start(offs_sb[:], offs)
         nc.sync.dma_start(
             scale_table[0:QUADRANT, :].bitcast(I32),
-            x_scales.rearrange("z q c -> q z c").bitcast(I32).to_broadcast([K // 32, 2, T // 4]),
+            x_scales.rearrange("z q c -> q z c").bitcast(I32).to_broadcast([BLOCKS, COPIES, T // PACK]),
         )
+        nc.sync.dma_start(offs_sb[:], offs)
         nc.sync.dma_start(w_raw[:], w1.rearrange("(p j) m -> p j m", j=PACK))
         nc.sync.dma_start(word_table[:], x_words[0].rearrange("p n t -> p (n t)").bitcast(I32))
         nc.sync.dma_start(cls_sb[:], cls)
@@ -56,19 +58,21 @@ def tile_picked_cbn_none_p_kernel(tc, x_words, x_scales, w1, gamma, beta, offs, 
         w_grouped = keep.tile([P, N, PACK], BF16, align_bytes=64)
         nc.scalar.copy(w_grouped[:], w_raw[:].rearrange("p j m -> p m j"))
 
-        for i, (a, b) in enumerate(((0, S // 2), (S // 2, S))):
-            picked = keep.tile([P, b - a], U8, align_bytes=64, name=f"picked{i}")
-            nc.vector.tensor_copy(picked[:], scale_table[:].indirect(offs_sb[:, a // STRIPE : b // STRIPE]))
+        def pick_scale_bytes(half):
+            start, end = half * S // COPIES, (half + 1) * S // COPIES
+            picked = keep.tile([P, end - start], U8, align_bytes=64, name=f"picked{half}")
+            nc.vector.tensor_copy(picked[:], scale_table[:].indirect(offs_sb[:, start // STRIPE : end // STRIPE]))
             for r in range(SCALE_ROWS):
                 nc.sync.dma_start(
-                    x_bytes[r:P:QUADRANT, a:b].bitcast(I32),
-                    picked[2 * r + i : QUADRANT : 8, :].bitcast(I32),
+                    x_bytes[r:P:QUADRANT, start:end].bitcast(I32),
+                    picked[COPIES * r + half : QUADRANT : COPIES * SCALE_ROWS, :].bitcast(I32),
                 )
-            if i == 0:
-                gamma_sb = keep.tile([P, U], F32, tag="w_then_gamma")
-                nc.sync.dma_start(gamma_sb[:], gamma)
 
-        beta_sb = keep.tile([P, U], F32, tag="early_then_beta")
+        pick_scale_bytes(0)
+        gamma_sb = keep.tile([P, U], F32, tag="w_then_gamma")
+        nc.sync.dma_start(gamma_sb[:], gamma)
+        pick_scale_bytes(1)
+        beta_sb = keep.tile([P, U], F32, tag="scales_then_beta")
         nc.sync.dma_start(beta_sb[:], beta)
 
         w_codes = keep.tile([P, N], U32, align_bytes=64)
@@ -76,26 +80,28 @@ def tile_picked_cbn_none_p_kernel(tc, x_words, x_scales, w1, gamma, beta, offs, 
         nc.vector.quantize_mx(w_codes[:].bitcast(FP8X4), w_bytes[:], w_grouped[:].rearrange("p m j -> p (m j)"))
 
         y = keep.tile([N, S], F32)
-        for i, (a, b) in enumerate(pieces):
+        for i, (start, end) in enumerate(pieces):
             x_codes = keep.tile([P, PIECE], U32, align_bytes=64, name=f"x_codes{i}")
-            nc.vector.tensor_copy(x_codes[:], word_table[:].bitcast(U32).indirect(offs_sb[:, a // STRIPE : b // STRIPE]))
+            nc.vector.tensor_copy(x_codes[:], word_table[:].bitcast(U32).indirect(offs_sb[:, start // STRIPE : end // STRIPE]))
             acc = psum.tile([N, PIECE], F32, name=f"acc{i}")
             nc.tensor.matmul_mx(
                 out=acc[:],
                 lhsT=w_codes[:].bitcast(FP8X4),
                 lhsT_scale=w_bytes[:],
                 rhs=x_codes[:].bitcast(FP8X4),
-                rhs_scale=x_bytes[:, a:b],
+                rhs_scale=x_bytes[:, start:end],
                 start=True,
                 stop=True,
             )
-            nc.scalar.copy(y[:, a:b], acc[:])
+            nc.scalar.copy(y[:, start:end], acc[:])
 
         scaled = keep.tile([N, S], F32)
-        for a, b in pieces:
-            nc.vector.tensor_tensor(scaled[:, a:b], gamma_sb[:].indirect(cls_sb[:, a // STRIPE : b // STRIPE]), y[:, a:b], MULT)
+        for start, end in pieces:
+            classes = cls_sb[:, start // STRIPE : end // STRIPE]
+            nc.vector.tensor_tensor(scaled[:, start:end], gamma_sb[:].indirect(classes), y[:, start:end], MULT)
 
         result = keep.tile([N, S], F32)
-        for a, b in SHIFTS:
-            nc.vector.tensor_tensor(result[:, a:b], beta_sb[:].indirect(cls_sb[:, a // STRIPE : b // STRIPE]), scaled[:, a:b], ADD)
-            nc.sync.dma_start(out[:, a:b], result[:, a:b])
+        for start, end in SHIFTS:
+            classes = cls_sb[:, start // STRIPE : end // STRIPE]
+            nc.vector.tensor_tensor(result[:, start:end], beta_sb[:].indirect(classes), scaled[:, start:end], ADD)
+            nc.sync.dma_start(out[:, start:end], result[:, start:end])

@@ -20,16 +20,19 @@ PACK = 4
 BLOCKS = K // 32
 QUADRANT = 32
 SCALE_ROWS = 4
-COPIES = QUADRANT // BLOCKS
 STRIPE = 16
 
-PIECE = 256
-SHIFTS = ((0, 512), (512, 768), (768, 896), (896, 1024))
+ROWS_AT = (112, 48)
+BYTE_PARTS = ((0, 384), (384, 1024),)
+WORD_PARTS = ((0, 512), (512, 1024),)
+PRODUCTS = ((0, 256), (256, 384), (384, 512), (512, 768), (768, 1024))
+SCALINGS = ((0, 384), (384, 512), (512, 768), (768, 1024),)
+SHIFTS = ((0, 512), (512, 768), (768, 896), (896, 1024),)
+QUANTISE_BEFORE = 1
 
 
 def tile_picked_cbn_none_p_kernel(tc, x_words, x_scales, w1, gamma, beta, offs, cls, out):
     nc = tc.nc
-    pieces = [(start, start + PIECE) for start in range(0, S, PIECE)]
 
     with ExitStack() as ctx:
         keep = ctx.enter_context(tc.tile_pool(name="keep", bufs=1))
@@ -38,38 +41,40 @@ def tile_picked_cbn_none_p_kernel(tc, x_words, x_scales, w1, gamma, beta, offs, 
         offs_sb = keep.tile([P, S // STRIPE], U16)
         cls_sb = keep.tile([P, S // STRIPE], U16)
         w_raw = keep.tile([P, PACK, N], F32, tag="w_then_gamma")
-        scale_table = keep.tile([P, T], U8, tag="scales_then_beta")
+        tables = [
+            keep.tile([P, T], U8, tag="scales_then_gamma", name="table0"),
+            keep.tile([P, T], U8, tag="scales_then_beta", name="table1"),
+        ]
         word_table = keep.tile([P, T], I32)
         x_bytes = keep.tile([P, S], U8, align_bytes=64)
 
-        nc.vector.memset(scale_table[QUADRANT : 2 * QUADRANT, :].bitcast(I32), 0)
-        nc.vector.memset(scale_table[2 * QUADRANT : P, :].bitcast(I32), 0)
+        nc.vector.memset(tables[0][0 : ROWS_AT[0], :].bitcast(I32), 0)
+        nc.vector.memset(tables[1][0 : ROWS_AT[1], :].bitcast(I32), 0)
+        nc.vector.memset(tables[1][ROWS_AT[1] + BLOCKS : P, :].bitcast(I32), 0)
         nc.vector.memset(x_bytes[:].bitcast(I32), 0)
 
-        nc.sync.dma_start(
-            scale_table[0:QUADRANT, :].bitcast(I32),
-            x_scales.rearrange("z q c -> q z c").bitcast(I32).to_broadcast([BLOCKS, COPIES, T // PACK]),
-        )
+        nc.sync.dma_start(tables[0][ROWS_AT[0] : ROWS_AT[0] + BLOCKS, :].bitcast(I32), x_scales[0].bitcast(I32))
         nc.sync.dma_start(offs_sb[:], offs)
-        nc.sync.dma_start(w_raw[:], w1.rearrange("(p j) m -> p j m", j=PACK))
+        nc.sync.dma_start(tables[1][ROWS_AT[1] : ROWS_AT[1] + BLOCKS, :].bitcast(I32), x_scales[0].bitcast(I32))
         nc.sync.dma_start(word_table[:], x_words[0].rearrange("p n t -> p (n t)").bitcast(I32))
+        nc.sync.dma_start(w_raw[:], w1.rearrange("(p j) m -> p j m", j=PACK))
         nc.sync.dma_start(cls_sb[:], cls)
 
-        w_grouped = keep.tile([P, N, PACK], BF16, align_bytes=64)
-        nc.scalar.copy(w_grouped[:], w_raw[:].rearrange("p j m -> p m j"))
+        w_grouped = keep.tile([P, N, PACK], BF16, align_bytes=64, tag="grouped_then_codes")
+        nc.scalar.copy(w_grouped[:].rearrange("p (c i) j -> p c j i", i=4), w_raw[:].rearrange("p j (c i) -> p c j i", i=4))
 
-        def pick_scale_bytes(half):
-            start, end = half * S // COPIES, (half + 1) * S // COPIES
-            picked = keep.tile([P, end - start], U8, align_bytes=64, name=f"picked{half}")
-            nc.vector.tensor_copy(picked[:], scale_table[:].indirect(offs_sb[:, start // STRIPE : end // STRIPE]))
+        def pick_scale_bytes(part):
+            start, end = BYTE_PARTS[part]
+            picked = keep.tile([P, end - start], U8, align_bytes=64, name=f"picked{part}")
+            nc.vector.tensor_copy(picked[:], tables[part][:].indirect(offs_sb[:, start // STRIPE : end // STRIPE]))
             for r in range(SCALE_ROWS):
                 nc.sync.dma_start(
                     x_bytes[r:P:QUADRANT, start:end].bitcast(I32),
-                    picked[COPIES * r + half : QUADRANT : COPIES * SCALE_ROWS, :].bitcast(I32),
+                    picked[ROWS_AT[part] + r : ROWS_AT[part] + BLOCKS : SCALE_ROWS, :].bitcast(I32),
                 )
 
         pick_scale_bytes(0)
-        gamma_sb = keep.tile([P, U], F32, tag="w_then_gamma")
+        gamma_sb = keep.tile([P, U], F32, tag="scales_then_gamma")
         nc.sync.dma_start(gamma_sb[:], gamma)
         pick_scale_bytes(1)
         beta_sb = keep.tile([P, U], F32, tag="scales_then_beta")
@@ -77,26 +82,35 @@ def tile_picked_cbn_none_p_kernel(tc, x_words, x_scales, w1, gamma, beta, offs, 
 
         w_codes = keep.tile([P, N], U32, align_bytes=64)
         w_bytes = keep.tile([P, N], U8, align_bytes=64)
-        nc.vector.quantize_mx(w_codes[:].bitcast(FP8X4), w_bytes[:], w_grouped[:].rearrange("p m j -> p (m j)"))
 
         y = keep.tile([N, S], F32)
-        for i, (start, end) in enumerate(pieces):
-            x_codes = keep.tile([P, PIECE], U32, align_bytes=64, name=f"x_codes{i}")
+        waiting = []
+        for i, (start, end) in enumerate(WORD_PARTS):
+            if i == QUANTISE_BEFORE:
+                nc.vector.quantize_mx(w_codes[:].bitcast(FP8X4), w_bytes[:], w_grouped[:].rearrange("p m j -> p (m j)"))
+            tag = "grouped_then_codes" if i == QUANTISE_BEFORE else f"codes{i}"
+            x_codes = keep.tile([P, end - start], U32, align_bytes=64, name=f"x_codes{i}", tag=tag)
             nc.vector.tensor_copy(x_codes[:], word_table[:].bitcast(U32).indirect(offs_sb[:, start // STRIPE : end // STRIPE]))
-            acc = psum.tile([N, PIECE], F32, name=f"acc{i}")
-            nc.tensor.matmul_mx(
-                out=acc[:],
-                lhsT=w_codes[:].bitcast(FP8X4),
-                lhsT_scale=w_bytes[:],
-                rhs=x_codes[:].bitcast(FP8X4),
-                rhs_scale=x_bytes[:, start:end],
-                start=True,
-                stop=True,
-            )
-            nc.scalar.copy(y[:, start:end], acc[:])
+            waiting.append((start, end, x_codes))
+            if i < QUANTISE_BEFORE:
+                continue
+            for first, last, codes in waiting:
+                for left, right in [piece for piece in PRODUCTS if first <= piece[0] < last]:
+                    acc = psum.tile([N, right - left], F32, name=f"acc{left}")
+                    nc.tensor.matmul_mx(
+                        out=acc[:],
+                        lhsT=w_codes[:].bitcast(FP8X4),
+                        lhsT_scale=w_bytes[:],
+                        rhs=codes[:, left - first : right - first].bitcast(FP8X4),
+                        rhs_scale=x_bytes[:, left:right],
+                        start=True,
+                        stop=True,
+                    )
+                    nc.scalar.copy(y[:, left:right], acc[:])
+            waiting = []
 
         scaled = keep.tile([N, S], F32)
-        for start, end in pieces:
+        for start, end in SCALINGS:
             classes = cls_sb[:, start // STRIPE : end // STRIPE]
             nc.vector.tensor_tensor(scaled[:, start:end], gamma_sb[:].indirect(classes), y[:, start:end], MULT)
 

@@ -26,7 +26,7 @@ ROWS_AT = (112, 48)
 BYTE_PARTS = ((0, 384), (384, 1024),)
 WORD_PARTS = ((0, 512), (512, 1024),)
 PRODUCTS = ((0, 256), (256, 384), (384, 512), (512, 768), (768, 1024))
-SCALINGS = ((0, 384), (384, 512), (512, 768), (768, 1024),)
+SCALINGS = ((0, 256), (256, 384), (384, 512), (512, 768), (768, 1024),)
 SHIFTS = ((0, 512), (512, 768), (768, 896), (896, 1024),)
 QUANTISE_BEFORE = 1
 
@@ -40,7 +40,7 @@ def tile_picked_cbn_none_p_kernel(tc, x_words, x_scales, w1, gamma, beta, offs, 
 
         offs_sb = keep.tile([P, S // STRIPE], U16)
         cls_sb = keep.tile([P, S // STRIPE], U16)
-        w_raw = keep.tile([P, PACK, N], F32, tag="w_then_gamma")
+        w_raw = keep.tile([P, PACK, N], F32, align_bytes=64, tag="raw_then_codes")
         tables = [
             keep.tile([P, T], U8, tag="scales_then_gamma", name="table0"),
             keep.tile([P, T], U8, tag="scales_then_beta", name="table1"),
@@ -60,7 +60,7 @@ def tile_picked_cbn_none_p_kernel(tc, x_words, x_scales, w1, gamma, beta, offs, 
         nc.sync.dma_start(w_raw[:], w1.rearrange("(p j) m -> p j m", j=PACK))
         nc.sync.dma_start(cls_sb[:], cls)
 
-        w_grouped = keep.tile([P, N, PACK], BF16, align_bytes=64, tag="grouped_then_codes")
+        w_grouped = keep.tile([P, N, PACK], BF16, align_bytes=64)
         nc.scalar.copy(w_grouped[:].rearrange("p (c i) j -> p c j i", i=4), w_raw[:].rearrange("p j (c i) -> p c j i", i=4))
 
         def pick_scale_bytes(part):
@@ -88,7 +88,7 @@ def tile_picked_cbn_none_p_kernel(tc, x_words, x_scales, w1, gamma, beta, offs, 
         for i, (start, end) in enumerate(WORD_PARTS):
             if i == QUANTISE_BEFORE:
                 nc.vector.quantize_mx(w_codes[:].bitcast(FP8X4), w_bytes[:], w_grouped[:].rearrange("p m j -> p (m j)"))
-            tag = "grouped_then_codes" if i == QUANTISE_BEFORE else f"codes{i}"
+            tag = "raw_then_codes" if i == QUANTISE_BEFORE else f"codes{i}"
             x_codes = keep.tile([P, end - start], U32, align_bytes=64, name=f"x_codes{i}", tag=tag)
             nc.vector.tensor_copy(x_codes[:], word_table[:].bitcast(U32).indirect(offs_sb[:, start // STRIPE : end // STRIPE]))
             waiting.append((start, end, x_codes))

@@ -25,9 +25,10 @@ STRIPE = 16
 ROWS_AT = (112, 48)
 BYTE_PARTS = ((0, 384), (384, 1024),)
 WORD_PARTS = ((0, 512), (512, 1024),)
-PRODUCTS = ((0, 256), (256, 384), (384, 512), (512, 768), (768, 1024))
-SCALINGS = ((0, 256), (256, 384), (384, 512), (512, 768), (768, 1024),)
+PRODUCTS = ((0, 128), (128, 384), (384, 512), (512, 640), (640, 768), (768, 1024))
+SCALINGS = ((0, 128), (128, 384), (640, 768), (384, 640), (768, 1024),)
 SHIFTS = ((0, 512), (512, 768), (768, 896), (896, 1024),)
+DIRECT = (640, 768)
 QUANTISE_BEFORE = 1
 
 
@@ -106,11 +107,19 @@ def tile_picked_cbn_none_p_kernel(tc, x_words, x_scales, w1, gamma, beta, offs, 
                         start=True,
                         stop=True,
                     )
-                    nc.scalar.copy(y[:, left:right], acc[:])
+                    if (left, right) == DIRECT:
+                        direct_acc = acc
+                    else:
+                        nc.scalar.copy(y[:, left:right], acc[:])
             waiting = []
 
         scaled = keep.tile([N, S], F32)
+        direct_gamma = keep.tile([N, DIRECT[1] - DIRECT[0]], F32)
+        nc.vector.tensor_copy(direct_gamma[:], gamma_sb[:].indirect(cls_sb[:, DIRECT[0] // STRIPE : DIRECT[1] // STRIPE]))
         for start, end in SCALINGS:
+            if (start, end) == DIRECT:
+                nc.vector.tensor_tensor(scaled[:, start:end], direct_acc[:], direct_gamma[:], MULT)
+                continue
             classes = cls_sb[:, start // STRIPE : end // STRIPE]
             nc.vector.tensor_tensor(scaled[:, start:end], gamma_sb[:].indirect(classes), y[:, start:end], MULT)
 

@@ -21,15 +21,14 @@ BLOCKS = K // 32
 QUADRANT = 32
 SCALE_ROWS = 4
 STRIPE = 16
+LINE = 4
 
-ROWS_AT = (112, 48)
-BYTE_PARTS = ((0, 384), (384, 1024),)
-WORD_PARTS = ((0, 512), (512, 1024),)
-PRODUCTS = ((0, 128), (128, 384), (384, 512), (512, 640), (640, 768), (768, 1024))
-SCALINGS = ((0, 128), (128, 384), (640, 768), (384, 640), (768, 1024),)
-SHIFTS = ((0, 512), (512, 768), (768, 896), (896, 1024),)
-DIRECT = (640, 768)
-QUANTISE_BEFORE = 1
+EARLY_BYTES, LATE_BYTES = (0, 384), (384, 1024)
+EARLY_ROWS, LATE_ROWS = 112, 48
+EARLY_WORDS, LATE_WORDS = (0, 640), (640, 1024)
+EARLY_PRODUCTS = ((0, 128), (128, 384), (384, 512), (512, 640))
+DIRECT, LAST_PRODUCT = (640, 768), (768, 1024)
+SHIFTS = ((0, 640), (640, 896), (896, 1024))
 
 
 def tile_picked_cbn_none_p_kernel(tc, x_words, x_scales, w1, gamma, beta, offs, cls, out):
@@ -42,89 +41,93 @@ def tile_picked_cbn_none_p_kernel(tc, x_words, x_scales, w1, gamma, beta, offs, 
         offs_sb = keep.tile([P, S // STRIPE], U16)
         cls_sb = keep.tile([P, S // STRIPE], U16)
         w_raw = keep.tile([P, PACK, N], F32, align_bytes=64, tag="raw_then_codes")
-        tables = [
-            keep.tile([P, T], U8, tag="scales_then_gamma", name="table0"),
-            keep.tile([P, T], U8, tag="scales_then_beta", name="table1"),
-        ]
+        early_table = keep.tile([P, T], U8, tag="scales_then_gamma")
+        late_table = keep.tile([P, T], U8, tag="scales_then_beta")
         word_table = keep.tile([P, T], I32)
         x_bytes = keep.tile([P, S], U8, align_bytes=64)
 
-        nc.vector.memset(tables[0][0 : ROWS_AT[0], :].bitcast(I32), 0)
-        nc.vector.memset(tables[1][0 : ROWS_AT[1], :].bitcast(I32), 0)
-        nc.vector.memset(tables[1][ROWS_AT[1] + BLOCKS : P, :].bitcast(I32), 0)
+        def entries(list_sb, start, end):
+            return list_sb[:, start // STRIPE : end // STRIPE]
+
+        nc.vector.memset(early_table[0:EARLY_ROWS, :].bitcast(I32), 0)
+        nc.vector.memset(late_table[0:LATE_ROWS, :].bitcast(I32), 0)
+        nc.vector.memset(late_table[LATE_ROWS + BLOCKS : P, :].bitcast(I32), 0)
         nc.vector.memset(x_bytes[:].bitcast(I32), 0)
 
-        nc.sync.dma_start(tables[0][ROWS_AT[0] : ROWS_AT[0] + BLOCKS, :].bitcast(I32), x_scales[0].bitcast(I32))
+        nc.sync.dma_start(early_table[EARLY_ROWS : EARLY_ROWS + BLOCKS, :].bitcast(I32), x_scales[0].bitcast(I32))
         nc.sync.dma_start(offs_sb[:], offs)
-        nc.sync.dma_start(tables[1][ROWS_AT[1] : ROWS_AT[1] + BLOCKS, :].bitcast(I32), x_scales[0].bitcast(I32))
+        nc.sync.dma_start(late_table[LATE_ROWS : LATE_ROWS + BLOCKS, :].bitcast(I32), x_scales[0].bitcast(I32))
         nc.sync.dma_start(word_table[:], x_words[0].rearrange("p n t -> p (n t)").bitcast(I32))
         nc.sync.dma_start(w_raw[:], w1.rearrange("(p j) m -> p j m", j=PACK))
         nc.sync.dma_start(cls_sb[:], cls)
 
         w_grouped = keep.tile([P, N, PACK], BF16, align_bytes=64)
-        nc.scalar.copy(w_grouped[:].rearrange("p (c i) j -> p c j i", i=4), w_raw[:].rearrange("p j (c i) -> p c j i", i=4))
+        nc.scalar.copy(
+            w_grouped[:].rearrange("p (c i) j -> p c j i", i=LINE),
+            w_raw[:].rearrange("p j (c i) -> p c j i", i=LINE),
+        )
 
-        def pick_scale_bytes(part):
-            start, end = BYTE_PARTS[part]
-            picked = keep.tile([P, end - start], U8, align_bytes=64, name=f"picked{part}")
-            nc.vector.tensor_copy(picked[:], tables[part][:].indirect(offs_sb[:, start // STRIPE : end // STRIPE]))
+        def pick_scale_bytes(table, first_row, start, end):
+            picked = keep.tile([P, end - start], U8, align_bytes=64, name=f"picked{start}")
+            nc.vector.tensor_copy(picked[:], table[:].indirect(entries(offs_sb, start, end)))
             for r in range(SCALE_ROWS):
                 nc.sync.dma_start(
                     x_bytes[r:P:QUADRANT, start:end].bitcast(I32),
-                    picked[ROWS_AT[part] + r : ROWS_AT[part] + BLOCKS : SCALE_ROWS, :].bitcast(I32),
+                    picked[first_row + r : first_row + BLOCKS : SCALE_ROWS, :].bitcast(I32),
                 )
 
-        pick_scale_bytes(0)
+        pick_scale_bytes(early_table, EARLY_ROWS, *EARLY_BYTES)
         gamma_sb = keep.tile([P, U], F32, tag="scales_then_gamma")
         nc.sync.dma_start(gamma_sb[:], gamma)
-        pick_scale_bytes(1)
+        pick_scale_bytes(late_table, LATE_ROWS, *LATE_BYTES)
         beta_sb = keep.tile([P, U], F32, tag="scales_then_beta")
         nc.sync.dma_start(beta_sb[:], beta)
 
         w_codes = keep.tile([P, N], U32, align_bytes=64)
         w_bytes = keep.tile([P, N], U8, align_bytes=64)
-
         y = keep.tile([N, S], F32)
-        waiting = []
-        for i, (start, end) in enumerate(WORD_PARTS):
-            if i == QUANTISE_BEFORE:
-                nc.vector.quantize_mx(w_codes[:].bitcast(FP8X4), w_bytes[:], w_grouped[:].rearrange("p m j -> p (m j)"))
-            tag = "raw_then_codes" if i == QUANTISE_BEFORE else f"codes{i}"
-            x_codes = keep.tile([P, end - start], U32, align_bytes=64, name=f"x_codes{i}", tag=tag)
-            nc.vector.tensor_copy(x_codes[:], word_table[:].bitcast(U32).indirect(offs_sb[:, start // STRIPE : end // STRIPE]))
-            waiting.append((start, end, x_codes))
-            if i < QUANTISE_BEFORE:
-                continue
-            for first, last, codes in waiting:
-                for left, right in [piece for piece in PRODUCTS if first <= piece[0] < last]:
-                    acc = psum.tile([N, right - left], F32, name=f"acc{left}")
-                    nc.tensor.matmul_mx(
-                        out=acc[:],
-                        lhsT=w_codes[:].bitcast(FP8X4),
-                        lhsT_scale=w_bytes[:],
-                        rhs=codes[:, left - first : right - first].bitcast(FP8X4),
-                        rhs_scale=x_bytes[:, left:right],
-                        start=True,
-                        stop=True,
-                    )
-                    if (left, right) == DIRECT:
-                        direct_acc = acc
-                    else:
-                        nc.scalar.copy(y[:, left:right], acc[:])
-            waiting = []
+
+        def pick_words(tag, start, end):
+            codes = keep.tile([P, end - start], U32, align_bytes=64, name=f"codes{start}", tag=tag)
+            nc.vector.tensor_copy(codes[:], word_table[:].bitcast(U32).indirect(entries(offs_sb, start, end)))
+            return codes
+
+        early_codes = pick_words("early_codes", *EARLY_WORDS)
+        nc.vector.quantize_mx(w_codes[:].bitcast(FP8X4), w_bytes[:], w_grouped[:].rearrange("p m j -> p (m j)"))
+        late_codes = pick_words("raw_then_codes", *LATE_WORDS)
+
+        def product(codes, first, start, end):
+            acc = psum.tile([N, end - start], F32, name=f"acc{start}")
+            nc.tensor.matmul_mx(
+                out=acc[:],
+                lhsT=w_codes[:].bitcast(FP8X4),
+                lhsT_scale=w_bytes[:],
+                rhs=codes[:, start - first : end - first].bitcast(FP8X4),
+                rhs_scale=x_bytes[:, start:end],
+                start=True,
+                stop=True,
+            )
+            return acc
+
+        for start, end in EARLY_PRODUCTS:
+            nc.scalar.copy(y[:, start:end], product(early_codes, EARLY_WORDS[0], start, end)[:])
+        direct_acc = product(late_codes, LATE_WORDS[0], *DIRECT)
+        nc.scalar.copy(y[:, LAST_PRODUCT[0] : LAST_PRODUCT[1]], product(late_codes, LATE_WORDS[0], *LAST_PRODUCT)[:])
 
         scaled = keep.tile([N, S], F32)
         direct_gamma = keep.tile([N, DIRECT[1] - DIRECT[0]], F32)
-        nc.vector.tensor_copy(direct_gamma[:], gamma_sb[:].indirect(cls_sb[:, DIRECT[0] // STRIPE : DIRECT[1] // STRIPE]))
-        for start, end in SCALINGS:
-            if (start, end) == DIRECT:
-                nc.vector.tensor_tensor(scaled[:, start:end], direct_acc[:], direct_gamma[:], MULT)
-                continue
-            classes = cls_sb[:, start // STRIPE : end // STRIPE]
-            nc.vector.tensor_tensor(scaled[:, start:end], gamma_sb[:].indirect(classes), y[:, start:end], MULT)
+
+        def scale(start, end):
+            nc.vector.tensor_tensor(scaled[:, start:end], gamma_sb[:].indirect(entries(cls_sb, start, end)), y[:, start:end], MULT)
+
+        nc.vector.tensor_copy(direct_gamma[:], gamma_sb[:].indirect(entries(cls_sb, *DIRECT)))
+        scale(*EARLY_PRODUCTS[0])
+        scale(*EARLY_PRODUCTS[1])
+        nc.vector.tensor_tensor(scaled[:, DIRECT[0] : DIRECT[1]], direct_acc[:], direct_gamma[:], MULT)
+        scale(LATE_BYTES[0], DIRECT[0])
+        scale(*LAST_PRODUCT)
 
         result = keep.tile([N, S], F32)
         for start, end in SHIFTS:
-            classes = cls_sb[:, start // STRIPE : end // STRIPE]
-            nc.vector.tensor_tensor(result[:, start:end], beta_sb[:].indirect(classes), scaled[:, start:end], ADD)
+            nc.vector.tensor_tensor(result[:, start:end], beta_sb[:].indirect(entries(cls_sb, start, end)), scaled[:, start:end], ADD)
             nc.sync.dma_start(out[:, start:end], result[:, start:end])

@@ -28,7 +28,7 @@ EARLY_ROWS, LATE_ROWS = 112, 48
 EARLY_WORDS, LATE_WORDS = (0, 640), (640, 1024)
 EARLY_PRODUCTS = ((0, 128), (128, 384), (384, 512), (512, 640))
 DIRECT, LAST_PRODUCT = (640, 768), (768, 1024)
-SHIFTS = ((0, 640), (640, 896), (896, 1024))
+SHIFTS = ((0, 512), (512, 768), (768, 896), (896, 1024))
 
 
 def tile_picked_cbn_none_p_kernel(tc, x_words, x_scales, w1, gamma, beta, offs, cls, out):

@@ -28,7 +28,7 @@ EARLY_ROWS, LATE_ROWS = 112, 48
 EARLY_WORDS, LATE_WORDS = (0, 640), (640, 1024)
 EARLY_PRODUCTS = ((0, 128), (128, 384), (384, 512), (512, 640))
 DIRECT, LAST_PRODUCT = (640, 768), (768, 1024)
-SHIFTS = ((0, 512), (512, 768), (768, 896), (896, 1024))
+SHIFTS = ((0, 384), (384, 704), (704, 896), (896, 1024))
 
 
 def tile_picked_cbn_none_p_kernel(tc, x_words, x_scales, w1, gamma, beta, offs, cls, out):

@@ -50,11 +50,11 @@ def tile_picked_cbn_none_p_kernel(tc, x_words, x_scales, w1, gamma, beta, offs, 
             return list_sb[:, start // STRIPE : end // STRIPE]
 
         nc.vector.memset(early_table[0:EARLY_ROWS, :].bitcast(I32), 0)
-        nc.vector.memset(late_table[0:LATE_ROWS, :].bitcast(I32), 0)
+        nc.vector.tensor_copy(late_table[0:LATE_ROWS, :].bitcast(I32), early_table[0:LATE_ROWS, :].bitcast(I32))
         nc.vector.memset(late_table[LATE_ROWS + BLOCKS : P, :].bitcast(I32), 0)
         nc.vector.memset(x_bytes[:].bitcast(I32), 0)
 
-        nc.sync.dma_start(early_table[EARLY_ROWS : EARLY_ROWS + BLOCKS, :].bitcast(I32), x_scales[0].bitcast(I32))
+        nc.scalar.dma_start(early_table[EARLY_ROWS : EARLY_ROWS + BLOCKS, :].bitcast(I32), x_scales[0].bitcast(I32))
         nc.sync.dma_start(offs_sb[:], offs)
         nc.sync.dma_start(late_table[LATE_ROWS : LATE_ROWS + BLOCKS, :].bitcast(I32), x_scales[0].bitcast(I32))
         nc.sync.dma_start(word_table[:], x_words[0].rearrange("p n t -> p (n t)").bitcast(I32))

@@ -14,6 +14,7 @@ U8 = mybir.dt.uint8
 FP8X4 = mybir.dt.float8_e4m3fn_x4
 MULT = mybir.AluOpType.mult
 ADD = mybir.AluOpType.add
+COPY = mybir.ActivationFunctionType.Copy
 
 P = 128
 PACK = 4
@@ -23,12 +24,12 @@ SCALE_ROWS = 4
 STRIPE = 16
 LINE = 4
 
-EARLY_BYTES, LATE_BYTES = (0, 384), (384, 1024)
-EARLY_ROWS, LATE_ROWS = 112, 48
-EARLY_WORDS, LATE_WORDS = (0, 640), (640, 1024)
-EARLY_PRODUCTS = ((0, 128), (128, 384), (384, 512), (512, 640))
-DIRECT, LAST_PRODUCT = (640, 768), (768, 1024)
-SHIFTS = ((0, 384), (384, 704), (704, 896), (896, 1024))
+TABLE_ROWS = 112
+WORDS = ((0, 512), (512, 1024))
+PRODUCTS = ((0, 256), (256, 512), (512, 768), (768, 1024))
+GAMMA_PICKS = ((0, 256), (256, 512), (512, 768), (768, 1024))
+FUSED_SHIFTS = ((0, 320),)
+BETA_PICKS = ((320, 640), (640, 896), (896, 1024))
 
 
 def tile_picked_cbn_none_p_kernel(tc, x_words, x_scales, w1, gamma, beta, offs, cls, out):
@@ -41,25 +42,23 @@ def tile_picked_cbn_none_p_kernel(tc, x_words, x_scales, w1, gamma, beta, offs, 
         offs_sb = keep.tile([P, S // STRIPE], U16)
         cls_sb = keep.tile([P, S // STRIPE], U16)
         w_raw = keep.tile([P, PACK, N], F32, align_bytes=64, tag="raw_then_codes")
-        early_table = keep.tile([P, T], U8, tag="scales_then_gamma")
-        late_table = keep.tile([P, T], U8, tag="scales_then_beta")
+        scale_table = keep.tile([P, T], U8, tag="scales_then_beta")
         word_table = keep.tile([P, T], I32)
+        gamma_sb = keep.tile([P, U], F32)
         x_bytes = keep.tile([P, S], U8, align_bytes=64)
 
         def entries(list_sb, start, end):
             return list_sb[:, start // STRIPE : end // STRIPE]
 
-        nc.vector.memset(early_table[0:EARLY_ROWS, :].bitcast(I32), 0)
-        nc.vector.tensor_copy(late_table[0:LATE_ROWS, :].bitcast(I32), early_table[0:LATE_ROWS, :].bitcast(I32))
-        nc.vector.memset(late_table[LATE_ROWS + BLOCKS : P, :].bitcast(I32), 0)
+        nc.vector.memset(scale_table[0:TABLE_ROWS, :].bitcast(I32), 0)
         nc.vector.memset(x_bytes[:].bitcast(I32), 0)
 
-        nc.scalar.dma_start(early_table[EARLY_ROWS : EARLY_ROWS + BLOCKS, :].bitcast(I32), x_scales[0].bitcast(I32))
+        nc.scalar.dma_start(scale_table[TABLE_ROWS:P, :].bitcast(I32), x_scales[0].bitcast(I32))
         nc.sync.dma_start(offs_sb[:], offs)
-        nc.sync.dma_start(late_table[LATE_ROWS : LATE_ROWS + BLOCKS, :].bitcast(I32), x_scales[0].bitcast(I32))
         nc.sync.dma_start(word_table[:], x_words[0].rearrange("p n t -> p (n t)").bitcast(I32))
         nc.sync.dma_start(w_raw[:], w1.rearrange("(p j) m -> p j m", j=PACK))
         nc.sync.dma_start(cls_sb[:], cls)
+        nc.sync.dma_start(gamma_sb[:], gamma)
 
         w_grouped = keep.tile([P, N, PACK], BF16, align_bytes=64)
         nc.scalar.copy(
@@ -67,36 +66,40 @@ def tile_picked_cbn_none_p_kernel(tc, x_words, x_scales, w1, gamma, beta, offs, 
             w_raw[:].rearrange("p j (c i) -> p c j i", i=LINE),
         )
 
-        def pick_scale_bytes(table, first_row, start, end):
-            picked = keep.tile([P, end - start], U8, align_bytes=64, name=f"picked{start}")
-            nc.vector.tensor_copy(picked[:], table[:].indirect(entries(offs_sb, start, end)))
-            for r in range(SCALE_ROWS):
-                nc.sync.dma_start(
-                    x_bytes[r:P:QUADRANT, start:end].bitcast(I32),
-                    picked[first_row + r : first_row + BLOCKS : SCALE_ROWS, :].bitcast(I32),
-                )
-
-        pick_scale_bytes(early_table, EARLY_ROWS, *EARLY_BYTES)
-        gamma_sb = keep.tile([P, U], F32, tag="scales_then_gamma")
-        nc.sync.dma_start(gamma_sb[:], gamma)
-        pick_scale_bytes(late_table, LATE_ROWS, *LATE_BYTES)
+        picked = keep.tile([P, S], U8, align_bytes=64)
+        nc.vector.tensor_copy(picked[:], scale_table[:].indirect(offs_sb[:]))
+        for r in range(SCALE_ROWS):
+            nc.sync.dma_start(
+                x_bytes[r:P:QUADRANT, :].bitcast(I32),
+                picked[TABLE_ROWS + r : P : SCALE_ROWS, :].bitcast(I32),
+            )
         beta_sb = keep.tile([P, U], F32, tag="scales_then_beta")
         nc.sync.dma_start(beta_sb[:], beta)
 
         w_codes = keep.tile([P, N], U32, align_bytes=64)
         w_bytes = keep.tile([P, N], U8, align_bytes=64)
-        y = keep.tile([N, S], F32)
 
         def pick_words(tag, start, end):
             codes = keep.tile([P, end - start], U32, align_bytes=64, name=f"codes{start}", tag=tag)
             nc.vector.tensor_copy(codes[:], word_table[:].bitcast(U32).indirect(entries(offs_sb, start, end)))
             return codes
 
-        early_codes = pick_words("early_codes", *EARLY_WORDS)
+        early_codes = pick_words("early_codes", *WORDS[0])
         nc.vector.quantize_mx(w_codes[:].bitcast(FP8X4), w_bytes[:], w_grouped[:].rearrange("p m j -> p (m j)"))
-        late_codes = pick_words("raw_then_codes", *LATE_WORDS)
+        late_codes = pick_words("raw_then_codes", *WORDS[1])
 
-        def product(codes, first, start, end):
+        gamma_picked = keep.tile([N, S], F32)
+        for start, end in GAMMA_PICKS:
+            nc.scalar.activation(gamma_picked[:, start:end], gamma_sb[:].indirect(entries(cls_sb, start, end)), COPY)
+        beta_picked = keep.tile([N, S], F32)
+        for start, end in BETA_PICKS:
+            nc.scalar.activation(beta_picked[:, start:end], beta_sb[:].indirect(entries(cls_sb, start, end)), COPY)
+
+        scaled = keep.tile([N, S], F32)
+        result = keep.tile([N, S], F32)
+
+        def scale(start, end):
+            codes, first = (early_codes, WORDS[0][0]) if end <= WORDS[0][1] else (late_codes, WORDS[1][0])
             acc = psum.tile([N, end - start], F32, name=f"acc{start}")
             nc.tensor.matmul_mx(
                 out=acc[:],
@@ -107,27 +110,15 @@ def tile_picked_cbn_none_p_kernel(tc, x_words, x_scales, w1, gamma, beta, offs, 
                 start=True,
                 stop=True,
             )
-            return acc
+            nc.vector.tensor_tensor(scaled[:, start:end], acc[:], gamma_picked[:, start:end], MULT)
 
-        for start, end in EARLY_PRODUCTS:
-            nc.scalar.copy(y[:, start:end], product(early_codes, EARLY_WORDS[0], start, end)[:])
-        direct_acc = product(late_codes, LATE_WORDS[0], *DIRECT)
-        nc.scalar.copy(y[:, LAST_PRODUCT[0] : LAST_PRODUCT[1]], product(late_codes, LATE_WORDS[0], *LAST_PRODUCT)[:])
-
-        scaled = keep.tile([N, S], F32)
-        direct_gamma = keep.tile([N, DIRECT[1] - DIRECT[0]], F32)
-
-        def scale(start, end):
-            nc.vector.tensor_tensor(scaled[:, start:end], gamma_sb[:].indirect(entries(cls_sb, start, end)), y[:, start:end], MULT)
-
-        nc.vector.tensor_copy(direct_gamma[:], gamma_sb[:].indirect(entries(cls_sb, *DIRECT)))
-        scale(*EARLY_PRODUCTS[0])
-        scale(*EARLY_PRODUCTS[1])
-        nc.vector.tensor_tensor(scaled[:, DIRECT[0] : DIRECT[1]], direct_acc[:], direct_gamma[:], MULT)
-        scale(LATE_BYTES[0], DIRECT[0])
-        scale(*LAST_PRODUCT)
-
-        result = keep.tile([N, S], F32)
-        for start, end in SHIFTS:
+        for start, end in PRODUCTS[:2]:
+            scale(start, end)
+        for start, end in FUSED_SHIFTS:
             nc.vector.tensor_tensor(result[:, start:end], beta_sb[:].indirect(entries(cls_sb, start, end)), scaled[:, start:end], ADD)
+            nc.sync.dma_start(out[:, start:end], result[:, start:end])
+        for start, end in PRODUCTS[2:]:
+            scale(start, end)
+        for start, end in BETA_PICKS:
+            nc.vector.tensor_tensor(result[:, start:end], beta_picked[:, start:end], scaled[:, start:end], ADD)
             nc.sync.dma_start(out[:, start:end], result[:, start:end])

@@ -25,11 +25,10 @@ STRIPE = 16
 LINE = 4
 
 TABLE_ROWS = 112
-WORDS = ((0, 512), (512, 1024))
-PRODUCTS = ((0, 256), (256, 512), (512, 768), (768, 1024))
-GAMMA_PICKS = ((0, 256), (256, 512), (512, 768), (768, 1024))
-FUSED_SHIFTS = ((0, 320),)
-BETA_PICKS = ((320, 640), (640, 896), (896, 1024))
+WORD_SPLIT = 640
+GAMMA_PICKS = ((0, 512), (512, 1024))
+SCALINGS = ((0, 256), (256, 512), (512, 768), (768, 1024))
+SHIFTS = ((0, 256), (256, 512), (512, 768), (768, 896), (896, 1024))
 
 
 def tile_picked_cbn_none_p_kernel(tc, x_words, x_scales, w1, gamma, beta, offs, cls, out):
@@ -42,9 +41,10 @@ def tile_picked_cbn_none_p_kernel(tc, x_words, x_scales, w1, gamma, beta, offs, 
         offs_sb = keep.tile([P, S // STRIPE], U16)
         cls_sb = keep.tile([P, S // STRIPE], U16)
         w_raw = keep.tile([P, PACK, N], F32, align_bytes=64, tag="raw_then_codes")
-        scale_table = keep.tile([P, T], U8, tag="scales_then_beta")
+        scale_table = keep.tile([P, T], U8)
         word_table = keep.tile([P, T], I32)
         gamma_sb = keep.tile([P, U], F32)
+        beta_sb = keep.tile([P, U], F32)
         x_bytes = keep.tile([P, S], U8, align_bytes=64)
 
         def entries(list_sb, start, end):
@@ -55,10 +55,20 @@ def tile_picked_cbn_none_p_kernel(tc, x_words, x_scales, w1, gamma, beta, offs, 
 
         nc.scalar.dma_start(scale_table[TABLE_ROWS:P, :].bitcast(I32), x_scales[0].bitcast(I32))
         nc.sync.dma_start(offs_sb[:], offs)
-        nc.sync.dma_start(word_table[:], x_words[0].rearrange("p n t -> p (n t)").bitcast(I32))
-        nc.sync.dma_start(w_raw[:], w1.rearrange("(p j) m -> p j m", j=PACK))
         nc.sync.dma_start(cls_sb[:], cls)
         nc.sync.dma_start(gamma_sb[:], gamma)
+        nc.sync.dma_start(word_table[:], x_words[0].rearrange("p n t -> p (n t)").bitcast(I32))
+        nc.sync.dma_start(w_raw[:], w1.rearrange("(p j) m -> p j m", j=PACK))
+        nc.sync.dma_start(beta_sb[:], beta)
+
+        warm_in = keep.tile([P, 1], F32)
+        warm_out = keep.tile([P, 1], F32)
+        nc.gpsimd.memset(warm_in[:], 0.0)
+        nc.scalar.activation(warm_out[:], warm_in[:], COPY)
+
+        gamma_picked = keep.tile([N, S], F32)
+        for start, end in GAMMA_PICKS:
+            nc.scalar.activation(gamma_picked[:, start:end], gamma_sb[:].indirect(entries(cls_sb, start, end)), COPY)
 
         w_grouped = keep.tile([P, N, PACK], BF16, align_bytes=64)
         nc.scalar.copy(
@@ -73,8 +83,6 @@ def tile_picked_cbn_none_p_kernel(tc, x_words, x_scales, w1, gamma, beta, offs, 
                 x_bytes[r:P:QUADRANT, :].bitcast(I32),
                 picked[TABLE_ROWS + r : P : SCALE_ROWS, :].bitcast(I32),
             )
-        beta_sb = keep.tile([P, U], F32, tag="scales_then_beta")
-        nc.sync.dma_start(beta_sb[:], beta)
 
         w_codes = keep.tile([P, N], U32, align_bytes=64)
         w_bytes = keep.tile([P, N], U8, align_bytes=64)
@@ -84,41 +92,45 @@ def tile_picked_cbn_none_p_kernel(tc, x_words, x_scales, w1, gamma, beta, offs, 
             nc.vector.tensor_copy(codes[:], word_table[:].bitcast(U32).indirect(entries(offs_sb, start, end)))
             return codes
 
-        early_codes = pick_words("early_codes", *WORDS[0])
+        early_codes = pick_words("early_codes", 0, WORD_SPLIT)
         nc.vector.quantize_mx(w_codes[:].bitcast(FP8X4), w_bytes[:], w_grouped[:].rearrange("p m j -> p (m j)"))
-        late_codes = pick_words("raw_then_codes", *WORDS[1])
+        late_codes = pick_words("raw_then_codes", WORD_SPLIT, S)
 
-        gamma_picked = keep.tile([N, S], F32)
-        for start, end in GAMMA_PICKS:
-            nc.scalar.activation(gamma_picked[:, start:end], gamma_sb[:].indirect(entries(cls_sb, start, end)), COPY)
         beta_picked = keep.tile([N, S], F32)
-        for start, end in BETA_PICKS:
+        for start, end in SHIFTS:
             nc.scalar.activation(beta_picked[:, start:end], beta_sb[:].indirect(entries(cls_sb, start, end)), COPY)
 
         scaled = keep.tile([N, S], F32)
         result = keep.tile([N, S], F32)
 
         def scale(start, end):
-            codes, first = (early_codes, WORDS[0][0]) if end <= WORDS[0][1] else (late_codes, WORDS[1][0])
             acc = psum.tile([N, end - start], F32, name=f"acc{start}")
-            nc.tensor.matmul_mx(
-                out=acc[:],
-                lhsT=w_codes[:].bitcast(FP8X4),
-                lhsT_scale=w_bytes[:],
-                rhs=codes[:, start - first : end - first].bitcast(FP8X4),
-                rhs_scale=x_bytes[:, start:end],
-                start=True,
-                stop=True,
-            )
+            for codes, first, lo, hi in (
+                (early_codes, 0, start, min(end, WORD_SPLIT)),
+                (late_codes, WORD_SPLIT, max(start, WORD_SPLIT), end),
+            ):
+                if lo < hi:
+                    nc.tensor.matmul_mx(
+                        out=acc[:, lo - start : hi - start],
+                        lhsT=w_codes[:].bitcast(FP8X4),
+                        lhsT_scale=w_bytes[:],
+                        rhs=codes[:, lo - first : hi - first].bitcast(FP8X4),
+                        rhs_scale=x_bytes[:, lo:hi],
+                        start=True,
+                        stop=True,
+                    )
             nc.vector.tensor_tensor(scaled[:, start:end], acc[:], gamma_picked[:, start:end], MULT)
 
-        for start, end in PRODUCTS[:2]:
-            scale(start, end)
-        for start, end in FUSED_SHIFTS:
-            nc.vector.tensor_tensor(result[:, start:end], beta_sb[:].indirect(entries(cls_sb, start, end)), scaled[:, start:end], ADD)
-            nc.sync.dma_start(out[:, start:end], result[:, start:end])
-        for start, end in PRODUCTS[2:]:
-            scale(start, end)
-        for start, end in BETA_PICKS:
+        def shift(start, end):
             nc.vector.tensor_tensor(result[:, start:end], beta_picked[:, start:end], scaled[:, start:end], ADD)
             nc.sync.dma_start(out[:, start:end], result[:, start:end])
+
+        scale(*SCALINGS[0])
+        scale(*SCALINGS[1])
+        shift(*SHIFTS[0])
+        scale(*SCALINGS[2])
+        shift(*SHIFTS[1])
+        scale(*SCALINGS[3])
+        shift(*SHIFTS[2])
+        shift(*SHIFTS[3])
+        shift(*SHIFTS[4])

@@ -26,7 +26,7 @@ LINE = 4
 
 TABLE_ROWS = 112
 WORD_SPLIT = 640
-GAMMA_PICKS = ((0, 512), (512, 1024))
+GAMMA_PICKS = ((0, 512), (512, 832))
 SCALINGS = ((0, 256), (256, 512), (512, 768), (768, 1024))
 SHIFTS = ((0, 256), (256, 512), (512, 768), (768, 896), (896, 1024))
 
@@ -83,6 +83,8 @@ def tile_picked_cbn_none_p_kernel(tc, x_words, x_scales, w1, gamma, beta, offs, 
                 x_bytes[r:P:QUADRANT, :].bitcast(I32),
                 picked[TABLE_ROWS + r : P : SCALE_ROWS, :].bitcast(I32),
             )
+
+        nc.vector.tensor_copy(gamma_picked[:, 832:1024], gamma_sb[:].indirect(entries(cls_sb, 832, 1024)))
 
         w_codes = keep.tile([P, N], U32, align_bytes=64)
         w_bytes = keep.tile([P, N], U8, align_bytes=64)

@@ -18,17 +18,11 @@ COPY = mybir.ActivationFunctionType.Copy
 
 P = 128
 PACK = 4
-BLOCKS = K // 32
 QUADRANT = 32
 SCALE_ROWS = 4
 STRIPE = 16
 LINE = 4
-
 TABLE_ROWS = 112
-WORD_SPLIT = 640
-GAMMA_PICKS = ((0, 512), (512, 832))
-SCALINGS = ((0, 256), (256, 512), (512, 768), (768, 1024))
-SHIFTS = ((0, 256), (256, 512), (512, 768), (768, 896), (896, 1024))
 
 
 def tile_picked_cbn_none_p_kernel(tc, x_words, x_scales, w1, gamma, beta, offs, cls, out):
@@ -67,72 +61,103 @@ def tile_picked_cbn_none_p_kernel(tc, x_words, x_scales, w1, gamma, beta, offs, 
         nc.scalar.activation(warm_out[:], warm_in[:], COPY)
 
         gamma_picked = keep.tile([N, S], F32)
-        for start, end in GAMMA_PICKS:
-            nc.scalar.activation(gamma_picked[:, start:end], gamma_sb[:].indirect(entries(cls_sb, start, end)), COPY)
-
+        beta_picked = keep.tile([N, S], F32)
+        scaled = keep.tile([N, S], F32)
+        result = keep.tile([N, S], F32)
         w_grouped = keep.tile([P, N, PACK], BF16, align_bytes=64)
-        nc.scalar.copy(
-            w_grouped[:].rearrange("p (c i) j -> p c j i", i=LINE),
-            w_raw[:].rearrange("p j (c i) -> p c j i", i=LINE),
-        )
-
         picked = keep.tile([P, S], U8, align_bytes=64)
-        nc.vector.tensor_copy(picked[:], scale_table[:].indirect(offs_sb[:]))
-        for r in range(SCALE_ROWS):
-            nc.sync.dma_start(
-                x_bytes[r:P:QUADRANT, :].bitcast(I32),
-                picked[TABLE_ROWS + r : P : SCALE_ROWS, :].bitcast(I32),
-            )
-
-        nc.vector.tensor_copy(gamma_picked[:, 832:1024], gamma_sb[:].indirect(entries(cls_sb, 832, 1024)))
-
         w_codes = keep.tile([P, N], U32, align_bytes=64)
         w_bytes = keep.tile([P, N], U8, align_bytes=64)
+        sums = {}
+
+        def pick_gamma(start, end):
+            nc.scalar.activation(gamma_picked[:, start:end], gamma_sb[:].indirect(entries(cls_sb, start, end)), COPY)
+
+        def pick_gamma_v(start, end):
+            nc.vector.tensor_copy(gamma_picked[:, start:end], gamma_sb[:].indirect(entries(cls_sb, start, end)))
+
+        def pick_beta(start, end):
+            nc.scalar.activation(beta_picked[:, start:end], beta_sb[:].indirect(entries(cls_sb, start, end)), COPY)
+
+        def round_w():
+            nc.scalar.copy(
+                w_grouped[:].rearrange("p (c i) j -> p c j i", i=LINE),
+                w_raw[:].rearrange("p j (c i) -> p c j i", i=LINE),
+            )
+
+        def pick_bytes():
+            nc.vector.tensor_copy(picked[:], scale_table[:].indirect(offs_sb[:]))
+            for r in range(SCALE_ROWS):
+                nc.sync.dma_start(
+                    x_bytes[r:P:QUADRANT, :].bitcast(I32),
+                    picked[TABLE_ROWS + r : P : SCALE_ROWS, :].bitcast(I32),
+                )
+
+        def quantize_w():
+            nc.vector.quantize_mx(w_codes[:].bitcast(FP8X4), w_bytes[:], w_grouped[:].rearrange("p m j -> p (m j)"))
 
         def pick_words(tag, start, end):
             codes = keep.tile([P, end - start], U32, align_bytes=64, name=f"codes{start}", tag=tag)
             nc.vector.tensor_copy(codes[:], word_table[:].bitcast(U32).indirect(entries(offs_sb, start, end)))
-            return codes
+            return codes, start
 
-        early_codes = pick_words("early_codes", 0, WORD_SPLIT)
-        nc.vector.quantize_mx(w_codes[:].bitcast(FP8X4), w_bytes[:], w_grouped[:].rearrange("p m j -> p (m j)"))
-        late_codes = pick_words("raw_then_codes", WORD_SPLIT, S)
+        def multiply(held, start, end, bank=None):
+            codes, first = held
+            if bank is None:
+                acc = psum.tile([N, end - start], F32, name=f"acc{start}")
+                sums[start] = acc
+                bank = start
+            nc.tensor.matmul_mx(
+                out=sums[bank][:, start - bank : end - bank],
+                lhsT=w_codes[:].bitcast(FP8X4),
+                lhsT_scale=w_bytes[:],
+                rhs=codes[:, start - first : end - first].bitcast(FP8X4),
+                rhs_scale=x_bytes[:, start:end],
+                start=True,
+                stop=True,
+            )
 
-        beta_picked = keep.tile([N, S], F32)
-        for start, end in SHIFTS:
-            nc.scalar.activation(beta_picked[:, start:end], beta_sb[:].indirect(entries(cls_sb, start, end)), COPY)
-
-        scaled = keep.tile([N, S], F32)
-        result = keep.tile([N, S], F32)
-
-        def scale(start, end):
+        def open_bank(start, end):
             acc = psum.tile([N, end - start], F32, name=f"acc{start}")
-            for codes, first, lo, hi in (
-                (early_codes, 0, start, min(end, WORD_SPLIT)),
-                (late_codes, WORD_SPLIT, max(start, WORD_SPLIT), end),
-            ):
-                if lo < hi:
-                    nc.tensor.matmul_mx(
-                        out=acc[:, lo - start : hi - start],
-                        lhsT=w_codes[:].bitcast(FP8X4),
-                        lhsT_scale=w_bytes[:],
-                        rhs=codes[:, lo - first : hi - first].bitcast(FP8X4),
-                        rhs_scale=x_bytes[:, lo:hi],
-                        start=True,
-                        stop=True,
-                    )
-            nc.vector.tensor_tensor(scaled[:, start:end], acc[:], gamma_picked[:, start:end], MULT)
+            sums[start] = acc
 
-        def shift(start, end):
-            nc.vector.tensor_tensor(result[:, start:end], beta_picked[:, start:end], scaled[:, start:end], ADD)
+        def scale(start, end, bank=None):
+            bank = start if bank is None else bank
+            nc.vector.tensor_tensor(scaled[:, start:end], sums[bank][:, start - bank : end - bank], gamma_picked[:, start:end], MULT)
+
+        def shift(engine, start, end):
+            engine.tensor_tensor(result[:, start:end], beta_picked[:, start:end], scaled[:, start:end], ADD)
             nc.sync.dma_start(out[:, start:end], result[:, start:end])
 
-        scale(*SCALINGS[0])
-        scale(*SCALINGS[1])
-        shift(*SHIFTS[0])
-        scale(*SCALINGS[2])
-        shift(*SHIFTS[1])
-        scale(*SCALINGS[3])
-        shift(*SHIFTS[2])
-        shift(*SHIFTS[3])
-        shift(*SHIFTS[4])
+        def shift_fused(start, end):
+            nc.vector.tensor_tensor(result[:, start:end], beta_sb[:].indirect(entries(cls_sb, start, end)), scaled[:, start:end], ADD)
+            nc.sync.dma_start(out[:, start:end], result[:, start:end])
+
+        pick_gamma(0, 512)
+        pick_gamma(512, 832)
+        round_w()
+        pick_bytes()
+        pick_gamma_v(832, 1024)
+        early = pick_words("early_codes", 0, 640)
+        quantize_w()
+        late = pick_words("raw_then_codes", 640, 1024)
+        pick_beta(0, 256)
+        pick_beta(256, 512)
+        pick_beta(512, 768)
+        pick_beta(768, 896)
+        pick_beta(896, 1024)
+        multiply(early, 0, 256)
+        scale(0, 256)
+        shift(nc.gpsimd, 0, 256)
+        multiply(early, 256, 512)
+        scale(256, 512)
+        open_bank(512, 768)
+        multiply(early, 512, 640, 512)
+        multiply(late, 640, 768, 512)
+        scale(512, 768)
+        multiply(late, 768, 1024)
+        scale(768, 1024)
+        shift(nc.vector, 256, 512)
+        shift(nc.vector, 512, 768)
+        shift(nc.vector, 768, 896)
+        shift(nc.vector, 896, 1024)

@@ -145,7 +145,6 @@ def tile_picked_cbn_none_p_kernel(tc, x_words, x_scales, w1, gamma, beta, offs, 
         pick_beta(256, 512)
         pick_beta(512, 768)
         pick_beta(768, 896)
-        pick_beta(896, 1024)
         multiply(early, 0, 256)
         scale(0, 256)
         shift(nc.gpsimd, 0, 256)
@@ -159,5 +158,5 @@ def tile_picked_cbn_none_p_kernel(tc, x_words, x_scales, w1, gamma, beta, offs, 
         scale(768, 1024)
         shift(nc.vector, 256, 512)
         shift(nc.vector, 512, 768)
+        shift_fused(896, 1024)
         shift(nc.vector, 768, 896)
-        shift(nc.vector, 896, 1024)

@@ -141,22 +141,22 @@ def tile_picked_cbn_none_p_kernel(tc, x_words, x_scales, w1, gamma, beta, offs, 
         early = pick_words("early_codes", 0, 640)
         quantize_w()
         late = pick_words("raw_then_codes", 640, 1024)
-        pick_beta(0, 256)
-        pick_beta(256, 512)
-        pick_beta(512, 768)
-        pick_beta(768, 896)
-        multiply(early, 0, 256)
-        scale(0, 256)
-        shift(nc.gpsimd, 0, 256)
-        multiply(early, 256, 512)
-        scale(256, 512)
-        open_bank(512, 768)
-        multiply(early, 512, 640, 512)
-        multiply(late, 640, 768, 512)
-        scale(512, 768)
-        multiply(late, 768, 1024)
-        scale(768, 1024)
-        shift(nc.vector, 256, 512)
-        shift(nc.vector, 512, 768)
-        shift_fused(896, 1024)
-        shift(nc.vector, 768, 896)
+        pick_beta(128, 384)
+        pick_beta(384, 640)
+        pick_beta(640, 896)
+        pick_beta(896, 1024)
+        multiply(early, 0, 128)
+        scale(0, 128)
+        multiply(early, 128, 384)
+        scale(128, 384)
+        shift_fused(0, 128)
+        shift(nc.gpsimd, 128, 384)
+        multiply(early, 384, 640)
+        scale(384, 640)
+        open_bank(640, 1024)
+        multiply(late, 640, 896, 640)
+        multiply(late, 896, 1024, 640)
+        scale(640, 1024)
+        shift(nc.vector, 384, 640)
+        shift(nc.vector, 640, 896)
+        shift(nc.vector, 896, 1024)

@@ -22,6 +22,7 @@ QUADRANT = 32
 SCALE_ROWS = 4
 STRIPE = 16
 LINE = 4
+ALIGN = 256
 TABLE_ROWS = 112
 
 
@@ -32,14 +33,14 @@ def tile_picked_cbn_none_p_kernel(tc, x_words, x_scales, w1, gamma, beta, offs, 
         keep = ctx.enter_context(tc.tile_pool(name="keep", bufs=1))
         psum = ctx.enter_context(tc.psum_pool(name="psum", bufs=1))
 
-        offs_sb = keep.tile([P, S // STRIPE], U16)
-        cls_sb = keep.tile([P, S // STRIPE], U16)
-        w_raw = keep.tile([P, PACK, N], F32, align_bytes=64, tag="raw_then_codes")
-        scale_table = keep.tile([P, T], U8)
-        word_table = keep.tile([P, T], I32)
-        gamma_sb = keep.tile([P, U], F32)
-        beta_sb = keep.tile([P, U], F32)
-        x_bytes = keep.tile([P, S], U8, align_bytes=64)
+        offs_sb = keep.tile([P, S // STRIPE], U16, align_bytes=ALIGN)
+        cls_sb = keep.tile([P, S // STRIPE], U16, align_bytes=ALIGN)
+        w_raw = keep.tile([P, PACK, N], F32, align_bytes=ALIGN, tag="raw_then_codes")
+        scale_table = keep.tile([P, T], U8, align_bytes=ALIGN)
+        word_table = keep.tile([P, T], I32, align_bytes=ALIGN)
+        gamma_sb = keep.tile([P, U], F32, align_bytes=ALIGN)
+        beta_sb = keep.tile([P, U], F32, align_bytes=ALIGN)
+        x_bytes = keep.tile([P, S], U8, align_bytes=ALIGN)
 
         def entries(list_sb, start, end):
             return list_sb[:, start // STRIPE : end // STRIPE]
@@ -60,14 +61,14 @@ def tile_picked_cbn_none_p_kernel(tc, x_words, x_scales, w1, gamma, beta, offs, 
         nc.gpsimd.memset(warm_in[:], 0.0)
         nc.scalar.activation(warm_out[:], warm_in[:], COPY)
 
-        gamma_picked = keep.tile([N, S], F32)
-        beta_picked = keep.tile([N, S], F32)
-        scaled = keep.tile([N, S], F32)
-        result = keep.tile([N, S], F32)
-        w_grouped = keep.tile([P, N, PACK], BF16, align_bytes=64)
-        picked = keep.tile([P, S], U8, align_bytes=64)
-        w_codes = keep.tile([P, N], U32, align_bytes=64)
-        w_bytes = keep.tile([P, N], U8, align_bytes=64)
+        gamma_picked = keep.tile([N, S], F32, align_bytes=ALIGN)
+        beta_picked = keep.tile([N, S], F32, align_bytes=ALIGN)
+        scaled = keep.tile([N, S], F32, align_bytes=ALIGN)
+        result = keep.tile([N, S], F32, align_bytes=ALIGN)
+        w_grouped = keep.tile([P, N, PACK], BF16, align_bytes=ALIGN)
+        picked = keep.tile([P, S], U8, align_bytes=ALIGN)
+        w_codes = keep.tile([P, N], U32, align_bytes=ALIGN)
+        w_bytes = keep.tile([P, N], U8, align_bytes=ALIGN)
         sums = {}
 
         def pick_gamma(start, end):
@@ -97,7 +98,7 @@ def tile_picked_cbn_none_p_kernel(tc, x_words, x_scales, w1, gamma, beta, offs, 
             nc.vector.quantize_mx(w_codes[:].bitcast(FP8X4), w_bytes[:], w_grouped[:].rearrange("p m j -> p (m j)"))
 
         def pick_words(tag, start, end):
-            codes = keep.tile([P, end - start], U32, align_bytes=64, name=f"codes{start}", tag=tag)
+            codes = keep.tile([P, end - start], U32, align_bytes=ALIGN, name=f"codes{start}", tag=tag)
             nc.vector.tensor_copy(codes[:], word_table[:].bitcast(U32).indirect(entries(offs_sb, start, end)))
             return codes, start
 

@@ -23,6 +23,7 @@ SCALE_ROWS = 4
 STRIPE = 16
 LINE = 4
 ALIGN = 256
+ROUND_SPLIT = 80
 TABLE_ROWS = 112
 
 
@@ -82,8 +83,11 @@ def tile_picked_cbn_none_p_kernel(tc, x_words, x_scales, w1, gamma, beta, offs, 
 
         def round_w():
             nc.scalar.copy(
-                w_grouped[:].rearrange("p (c i) j -> p c j i", i=LINE),
-                w_raw[:].rearrange("p j (c i) -> p c j i", i=LINE),
+                w_grouped[:, 0:ROUND_SPLIT, :].rearrange("p (c i) j -> p c j i", i=LINE),
+                w_raw[:, :, 0:ROUND_SPLIT].rearrange("p j (c i) -> p c j i", i=LINE),
+            )
+            nc.gpsimd.tensor_scalar(
+                w_grouped[:, ROUND_SPLIT:N, :], w_raw[:, :, ROUND_SPLIT:N].rearrange("p j m -> p m j"), 1.0, 0.0, MULT, ADD
             )
 
         def pick_bytes():

from contextlib import ExitStack

import concourse.mybir as mybir

K, T, S, N, U = 512, 2048, 1024, 128, 1024
FLOPS = 2 * K * N * S

F32 = mybir.dt.float32
BF16 = mybir.dt.bfloat16
I32 = mybir.dt.int32
U32 = mybir.dt.uint32
U16 = mybir.dt.uint16
U8 = mybir.dt.uint8
FP8X4 = mybir.dt.float8_e4m3fn_x4
MULT = mybir.AluOpType.mult
ADD = mybir.AluOpType.add
COPY = mybir.ActivationFunctionType.Copy

P = 128
PACK = 4
QUADRANT = 32
SCALE_ROWS = 4
STRIPE = 16
LINE = 4
ALIGN = 256
ROUND_SPLIT = 80
TABLE_ROWS = 112


def tile_picked_cbn_none_p_kernel(tc, x_words, x_scales, w1, gamma, beta, offs, cls, out):
    nc = tc.nc

    with ExitStack() as ctx:
        keep = ctx.enter_context(tc.tile_pool(name="keep", bufs=1))
        psum = ctx.enter_context(tc.psum_pool(name="psum", bufs=1))

        offs_sb = keep.tile([P, S // STRIPE], U16, align_bytes=ALIGN)
        cls_sb = keep.tile([P, S // STRIPE], U16, align_bytes=ALIGN)
        w_raw = keep.tile([P, PACK, N], F32, align_bytes=ALIGN, tag="raw_then_codes")
        scale_table = keep.tile([P, T], U8, align_bytes=ALIGN)
        word_table = keep.tile([P, T], I32, align_bytes=ALIGN)
        gamma_sb = keep.tile([P, U], F32, align_bytes=ALIGN)
        beta_sb = keep.tile([P, U], F32, align_bytes=ALIGN)
        x_bytes = keep.tile([P, S], U8, align_bytes=ALIGN)

        def entries(list_sb, start, end):
            return list_sb[:, start // STRIPE : end // STRIPE]

        nc.vector.memset(scale_table[0:TABLE_ROWS, :].bitcast(I32), 0)
        nc.vector.memset(x_bytes[:].bitcast(I32), 0)

        nc.scalar.dma_start(scale_table[TABLE_ROWS:P, :].bitcast(I32), x_scales[0].bitcast(I32))
        nc.sync.dma_start(offs_sb[:], offs)
        nc.sync.dma_start(cls_sb[:], cls)
        nc.sync.dma_start(gamma_sb[:], gamma)
        nc.sync.dma_start(word_table[:], x_words[0].rearrange("p n t -> p (n t)").bitcast(I32))
        nc.sync.dma_start(w_raw[:], w1.rearrange("(p j) m -> p j m", j=PACK))
        nc.sync.dma_start(beta_sb[:], beta)

        warm_in = keep.tile([P, 1], F32)
        warm_out = keep.tile([P, 1], F32)
        nc.gpsimd.memset(warm_in[:], 0.0)
        nc.scalar.activation(warm_out[:], warm_in[:], COPY)

        gamma_picked = keep.tile([N, S], F32, align_bytes=ALIGN)
        beta_picked = keep.tile([N, S], F32, align_bytes=ALIGN)
        scaled = keep.tile([N, S], F32, align_bytes=ALIGN)
        result = keep.tile([N, S], F32, align_bytes=ALIGN)
        w_grouped = keep.tile([P, N, PACK], BF16, align_bytes=ALIGN)
        picked = keep.tile([P, S], U8, align_bytes=ALIGN)
        w_codes = keep.tile([P, N], U32, align_bytes=ALIGN)
        w_bytes = keep.tile([P, N], U8, align_bytes=ALIGN)
        sums = {}

        def pick_gamma(start, end):
            nc.scalar.activation(gamma_picked[:, start:end], gamma_sb[:].indirect(entries(cls_sb, start, end)), COPY)

        def pick_gamma_v(start, end):
            nc.vector.tensor_copy(gamma_picked[:, start:end], gamma_sb[:].indirect(entries(cls_sb, start, end)))

        def pick_beta(start, end):
            nc.scalar.activation(beta_picked[:, start:end], beta_sb[:].indirect(entries(cls_sb, start, end)), COPY)

        def round_w():
            nc.scalar.copy(
                w_grouped[:, 0:ROUND_SPLIT, :].rearrange("p (c i) j -> p c j i", i=LINE),
                w_raw[:, :, 0:ROUND_SPLIT].rearrange("p j (c i) -> p c j i", i=LINE),
            )
            nc.gpsimd.tensor_scalar(
                w_grouped[:, ROUND_SPLIT:N, :], w_raw[:, :, ROUND_SPLIT:N].rearrange("p j m -> p m j"), 1.0, 0.0, MULT, ADD
            )

        def pick_bytes():
            nc.vector.tensor_copy(picked[:], scale_table[:].indirect(offs_sb[:]))
            for r in range(SCALE_ROWS):
                nc.sync.dma_start(
                    x_bytes[r:P:QUADRANT, :].bitcast(I32),
                    picked[TABLE_ROWS + r : P : SCALE_ROWS, :].bitcast(I32),
                )

        def quantize_w():
            nc.vector.quantize_mx(w_codes[:].bitcast(FP8X4), w_bytes[:], w_grouped[:].rearrange("p m j -> p (m j)"))

        def pick_words(tag, start, end):
            codes = keep.tile([P, end - start], U32, align_bytes=ALIGN, name=f"codes{start}", tag=tag)
            nc.vector.tensor_copy(codes[:], word_table[:].bitcast(U32).indirect(entries(offs_sb, start, end)))
            return codes, start

        def multiply(held, start, end, bank=None):
            codes, first = held
            if bank is None:
                acc = psum.tile([N, end - start], F32, name=f"acc{start}")
                sums[start] = acc
                bank = start
            nc.tensor.matmul_mx(
                out=sums[bank][:, start - bank : end - bank],
                lhsT=w_codes[:].bitcast(FP8X4),
                lhsT_scale=w_bytes[:],
                rhs=codes[:, start - first : end - first].bitcast(FP8X4),
                rhs_scale=x_bytes[:, start:end],
                start=True,
                stop=True,
            )

        def open_bank(start, end):
            acc = psum.tile([N, end - start], F32, name=f"acc{start}")
            sums[start] = acc

        def scale(start, end, bank=None):
            bank = start if bank is None else bank
            nc.vector.tensor_tensor(scaled[:, start:end], sums[bank][:, start - bank : end - bank], gamma_picked[:, start:end], MULT)

        def shift(engine, start, end):
            engine.tensor_tensor(result[:, start:end], beta_picked[:, start:end], scaled[:, start:end], ADD)
            nc.sync.dma_start(out[:, start:end], result[:, start:end])

        def shift_fused(start, end):
            nc.vector.tensor_tensor(result[:, start:end], beta_sb[:].indirect(entries(cls_sb, start, end)), scaled[:, start:end], ADD)
            nc.sync.dma_start(out[:, start:end], result[:, start:end])

        pick_gamma(0, 512)
        pick_gamma(512, 832)
        round_w()
        pick_bytes()
        pick_gamma_v(832, 1024)
        early = pick_words("early_codes", 0, 640)
        quantize_w()
        late = pick_words("raw_then_codes", 640, 1024)
        pick_beta(128, 384)
        pick_beta(384, 640)
        pick_beta(640, 896)
        pick_beta(896, 1024)
        multiply(early, 0, 128)
        scale(0, 128)
        multiply(early, 128, 384)
        scale(128, 384)
        shift_fused(0, 128)
        shift(nc.gpsimd, 128, 384)
        multiply(early, 384, 640)
        scale(384, 640)
        open_bank(640, 1024)
        multiply(late, 640, 896, 640)
        multiply(late, 896, 1024, 640)
        scale(640, 1024)
        shift(nc.vector, 384, 640)
        shift(nc.vector, 640, 896)
        shift(nc.vector, 896, 1024)
